import numpy as np
import ml_dtypes


def mxq(x, axis, fmt="e4m3"):
    dtype, down = {"e4m3": (ml_dtypes.float8_e4m3fn, 7), "e5m2": (ml_dtypes.float8_e5m2, 14)}[fmt]
    v = np.moveaxis(np.asarray(x, np.float32).astype(ml_dtypes.bfloat16).astype(np.float64), axis, -1)
    blocks = v.reshape(v.shape[:-1] + (-1, 32))
    amax = np.abs(blocks).max(-1, keepdims=True)
    byte = np.maximum(np.where(amax > 0, np.frexp(amax)[1] - 1 + 127, 0) - down, 1)
    scale = np.exp2(byte - 127.0)
    codes = (blocks / scale).astype(np.float32).astype(dtype).astype(np.float64)
    return np.moveaxis((codes * scale).reshape(v.shape), -1, axis)


WIDE = False


def mx_kscale(k):
    if not WIDE:
        return np.ones(k)
    levels = np.array([10, -10, 5, -5, 0])
    if k % 512:
        return np.exp2(np.random.permutation(np.resize(levels, k // 32))).repeat(32)
    a = np.empty((k // 512, 16))
    for p in range(k // 512):
        a[p, :8] = np.random.permutation(np.resize(levels, 8))
        for g in range(8):
            far = levels[np.abs(levels - a[p, g]) >= 10]
            a[p, g + 8] = far[np.random.randint(len(far))]
    return np.exp2(a.ravel()).repeat(32)


BF16 = ml_dtypes.bfloat16


def bf(x):
    return np.asarray(x, np.float32).astype(BF16)


def f64(x):
    return np.asarray(x).astype(np.float64)


E2M1 = np.array([0.0, 0.5, 1.0, 1.5, 2.0, 3.0, 4.0, 6.0, -0.0, -0.5, -1.0, -1.5, -2.0, -3.0, -4.0, -6.0])


def pack_weight(w, fmt):
    k, n = w.shape
    w = f64(bf(w)).reshape(k // 32, 32, n)
    amax = np.abs(w).max(1)
    if fmt == "e4m3":
        byte = np.frexp(amax)[1] - 1 + 127 - 7
    else:
        mant, ex = np.frexp(amax / 6.0)
        byte = np.where(mant > 0.5, ex, ex - 1) + 127
    byte = np.clip(np.where(amax > 0, byte, 1), 1, 254)
    scaled = (w * np.exp2(127.0 - byte)[:, None, :]).reshape(k, n).astype(np.float32)
    by_word = np.ascontiguousarray(scaled.reshape(k // 512, 128, 4, n).transpose(0, 1, 3, 2))
    if fmt == "e4m3":
        words = by_word.astype(ml_dtypes.float8_e4m3fn).view(np.uint8)
    else:
        c = by_word.astype(ml_dtypes.float4_e2m1fn).view(np.uint8) & 0xF
        words = c[..., 0::2] | (c[..., 1::2] << 4)
    return np.ascontiguousarray(words), np.ascontiguousarray(byte.astype(np.uint8).reshape(k // 512, 16, n))


def unpack_weight(words, scales, fmt):
    g, p, n, _ = words.shape
    if fmt == "e4m3":
        vals = np.ascontiguousarray(words).view(ml_dtypes.float8_e4m3fn).astype(np.float64)
    else:
        nib = np.empty((g, p, n, 4), np.uint8)
        nib[..., 0::2] = words & 0xF
        nib[..., 1::2] = words >> 4
        vals = E2M1[nib]
    vals = vals * np.repeat(np.exp2(scales.astype(np.float64) - 127.0), 8, axis=1)[..., None]
    return vals.transpose(0, 1, 3, 2).reshape(g * 512, n)
def pack4(w):
    words, scales = pack_weight(w, "e2m1")
    return words.reshape(words.shape[0], 128, -1), scales


def unpack4(words, scales):
    return unpack_weight(words.reshape(words.shape[0], 128, -1, 2), scales, "e2m1")


def planes(Y):
    n, m = Y.shape
    b = f64(bf(Y)).reshape(n // 32, 32, m)
    amax = np.abs(b).max(1)
    byte = np.clip(np.where(amax > 0, np.frexp(amax)[1] - 1 + 127 - 7, 1), 1, 254)
    codes = (b * np.exp2(127.0 - byte)[:, None, :]).reshape(n, m).astype(np.float32).astype(ml_dtypes.float8_e4m3fn).view(np.uint8)
    words = codes.reshape(n // 512, 128, 4, m).transpose(0, 1, 3, 2)
    return np.ascontiguousarray(words), np.ascontiguousarray(byte.astype(np.uint8).reshape(n // 512, 16, m))


D, O, S, K, C = 1024, 2048, 512, 1024, 512

def setup_inputs():
    rnd = np.random.randn
    sk, sc, t = mx_kscale(K)[:, None], mx_kscale(C)[:, None], mx_kscale(O)
    dest_words, dest_scales = pack_weight(rnd(K, D) * sk, "e4m3")
    load_words, load_scales = pack4(rnd(C, O) / np.sqrt(C) * sc)
    return {
        "dest_words": dest_words, "dest_scales": dest_scales,
        "origin_feat": bf(0.8 * rnd(K, O) / np.sqrt(K) / sk),
        "load_words": load_words, "load_scales": load_scales,
        "drivers": bf(rnd(C, S) / sc),
        "mass": bf(0.5 * np.exp(0.5 * rnd(O)) / np.sqrt(O) * t),
        "amplitude": bf(np.exp(0.3 * rnd(O)) / t),
        "common": bf(0.4 * rnd(O) / t),
        "outside": bf(0.4 * rnd(S)),
        "receptivity": bf(np.exp(0.8 * rnd(D))),
    }

def reference(dest_words, dest_scales, origin_feat, load_words, load_scales, drivers, mass, amplitude, common, outside, receptivity):
    dest = unpack_weight(dest_words, dest_scales, "e4m3")
    load = unpack4(load_words, load_scales)
    flow = np.exp(dest.T @ mxq(f64(origin_feat), 0, "e4m3")) * f64(mass)[None, :]
    prev = (load.T @ mxq(f64(drivers), 0, "e4m3")) * f64(amplitude)[:, None] + f64(common)[:, None]
    imported = mxq(flow, 1, "e4m3") @ mxq(prev, 0, "e4m3")
    y = (imported + f64(outside)[None, :]) * f64(receptivity)[:, None]
    Y = y.reshape(D, S)
    words, scales = planes(Y)
    return y, words, scales

@@ -1,0 +1,286 @@
+from contextlib import ExitStack
+
+import concourse.mybir as mybir
+from concourse.masks import make_identity
+
+D, O, S, K, C = 1024, 2048, 512, 1024, 512
+FLOPS = 2 * D * O * K + 2 * O * S * C + 2 * D * S * O
+
+F32 = mybir.dt.float32
+BF16 = mybir.dt.bfloat16
+I32 = mybir.dt.int32
+U32 = mybir.dt.uint32
+U8 = mybir.dt.uint8
+FP8X4 = mybir.dt.float8_e4m3fn_x4
+FP4X4 = mybir.dt.float4_e2m1fn_x4
+ACT = mybir.ActivationFunctionType
+ALU = mybir.AluOpType
+
+P = 128
+W = 512
+LN2 = 0.6931471805599453
+
+SCHEDULE = [('IB', 0, 0, 'V'), ('vperm',), ('IZ', 'V'), ('vtr',), ('vch1',), ('QZ',), ('LPw',), ('LPs',), ('ln',), ('mP', 0), ('vch3',), ('QB', 0, 0), ('vch2',), ('IB', 0, 1, 'S'), ('QB', 0, 1), ('IB', 1, 0, 'V'), ('eP', 0, 'S'), ('IB', 1, 1, 'V'), ('mP', 1), ('eP', 1, 'S'), ('QB', 1, 0), ('QB', 1, 1), ('mF', 0, 0), ('IB', 2, 0, 'V'), ('eF', 0, 0), ('mF', 0, 1), ('IP', 0, 'V'), ('eF', 0, 1), ('mF', 1, 0), ('IP', 1, 'V'), ('IB', 3, 0, 'V'), ('eF', 1, 0), ('IB', 2, 1, 'V'), ('IF', 0, 0, 'V'), ('mP', 2), ('QB', 2, 1), ('QF', 0, 0), ('eP', 2, 'S'), ('QB', 2, 0), ('mF', 2, 0), ('IB', 3, 1, 'V'), ('QP', 0), ('mY', 0, 0), ('IF', 0, 1, 'V'), ('QP', 1), ('QB', 3, 1), ('eF', 2, 0), ('QB', 3, 0), ('mP', 3), ('OR', 0, 'V'), ('IP', 2, 'V'), ('eP', 3, 'S'), ('mF', 3, 0), ('eF', 3, 0), ('IP', 3, 'V'), ('IF', 1, 0, 'V'), ('mF', 1, 1), ('IF', 2, 0, 'V'), ('QF', 1, 0), ('eF', 1, 1), ('QF', 2, 0), ('mF', 2, 1), ('eF', 2, 1), ('QF', 0, 1), ('mY', 1, 0), ('IF', 3, 0, 'V'), ('QP', 2), ('IF', 2, 1, 'V'), ('QF', 3, 0), ('QP', 3), ('mF', 3, 1), ('IF', 1, 1, 'S'), ('mY', 2, 0), ('mY', 3, 0), ('eF', 3, 1), ('QF', 1, 1), ('st', 0, 0, 'V'), ('st', 0, 1, 'V'), ('IF', 3, 1, 'S'), ('mY', 0, 1), ('mY', 1, 1), ('QF', 2, 1), ('mY', 2, 1), ('OR', 1, 'S'), ('IY', 0, 0, 'V'), ('IY', 0, 1, 'V'), ('QF', 3, 1), ('QY', 0, 1), ('QY', 0, 0), ('mY', 3, 1), ('st', 1, 0, 'V'), ('st', 1, 1, 'V'), ('IY', 1, 1, 'V'), ('IY', 1, 0, 'S'), ('QY', 1, 1), ('QY', 1, 0)]
+
+
+def tile_gravity_mobility_importation_k4_kernel(
+    tc, dest_words, dest_scales, origin_feat, load_words, load_scales, drivers,
+    mass, amplitude, common, outside, receptivity, out_0, out_1, out_2,
+):
+    nc = tc.nc
+    with ExitStack() as ctx:
+        keep = ctx.enter_context(tc.tile_pool(name="keep", bufs=1))
+        turn = ctx.enter_context(tc.tile_pool(name="turn", bufs=1))
+        psum = ctx.enter_context(tc.psum_pool(name="psum", bufs=1))
+        ctx.enter_context(tc.manual_schedule())
+
+        def kept(name, shape, dtype):
+            return keep.tile(shape, dtype, name=name, align_bytes=64)
+
+        rows_in = kept("rows_in", [P, W], BF16)
+        rows_perm = kept("rows_perm", [P, 4, P], BF16)
+        ident = kept("ident", [P, P], BF16)
+        vec = kept("vec", [P, 3, 16], F32)
+        mant = kept("mant", [P, 16], I32)
+        expo = kept("expo", [P, 16], I32)
+        twice_pos = kept("twice_pos", [P, 16], F32)
+        signed = kept("signed", [P, 2, 16], F32)
+        ln_pow = kept("ln_pow", [P, 16], F32)
+        ln_zero = kept("ln_zero", [P, 16], F32)
+        ln_base = kept("ln_base", [P, 16], F32)
+        ln_mant = kept("ln_mant", [P, 16], F32)
+        ln_mass = kept("ln_mass", [P, 16], F32)
+        recept_in = kept("recept_in", [P, 2, 4], BF16)
+        recept = kept("recept", [P, 2, 4], F32)
+        outside_all = kept("outside_all", [P, S], BF16)
+        offset = kept("offset", [P, 2, 4, S], F32)
+        l_words_in = kept("l_words_in", [P, 2 * O], U8)
+        l_words = kept("l_words", [P, 2 * O], U8)
+        l_scales_in = kept("l_scales_in", [P, O], U8)
+        l_scales = kept("l_scales", [P, O], U8)
+        a_words = [kept("a_words%d" % G, [P, 2, W], U32) for G in range(2)]
+        a_scales = kept("a_scales", [P, 2, D], U8)
+        z_rows = kept("z_rows", [P, 4, S], BF16)
+        b_rows = {(g, c): kept("b_rows%d%d" % (g, c), [P, 4, W], BF16) for g in range(4) for c in range(2)}
+        y = [kept("y%d" % G, [P, 4, S], F32) for G in range(2)]
+        codes = {}
+        scales = {}
+        for key in (["z"] + [("b", g, c) for g in range(4) for c in range(2)] + [("p", g) for g in range(4)]
+                    + [("f", g, G) for g in range(4) for G in range(2)] + [("y", G) for G in range(2)]):
+            label = "".join(str(x) for x in key)
+            codes[key] = kept("codes_" + label, [P, W], U32)
+            scales[key] = kept("scales_" + label, [P, W], U8)
+        grouped = {}
+        evac = {}
+        bank = {}
+
+        nc.vector.memset(rows_in[:].bitcast(I32), 0)
+        nc.vector.memset(l_scales_in[:].bitcast(I32), 0)
+        nc.gpsimd.memset(a_scales[:].bitcast(I32), 0)
+        make_identity(nc, ident[:])
+
+        def load_b(g, c):
+            nc.sync.dma_start(
+                out=b_rows[g, c][:],
+                in_=origin_feat[c * W : (c + 1) * W, g * W : (g + 1) * W].rearrange("(p j) o -> p j o", j=4),
+            )
+
+        def load_a(G):
+            nc.sync.dma_start(
+                out=a_words[G][:].bitcast(I32),
+                in_=dest_words.rearrange("c p n t -> p c (n t)")[:, :, G * 4 * W : (G + 1) * 4 * W].bitcast(I32),
+            )
+
+        load_b(0, 0)
+        for v, vector_in in enumerate((mass, amplitude, common)):
+            nc.sync.dma_start(out=rows_in[4 * v : 4 * v + 4, :], in_=vector_in.rearrange("(g x) -> g x", g=4))
+        nc.sync.dma_start(out=z_rows[:], in_=drivers.rearrange("(p j) s -> p j s", j=4))
+        load_b(0, 1)
+        nc.sync.dma_start(out=l_words_in[:].bitcast(I32), in_=load_words[0].bitcast(I32))
+        for q in range(4):
+            nc.sync.dma_start(
+                out=l_scales_in[32 * q : 32 * q + 4, :].bitcast(I32),
+                in_=load_scales[0, 4 * q : 4 * q + 4, :].bitcast(I32),
+            )
+        load_a(0)
+        for q in range(4):
+            nc.sync.dma_start(
+                out=a_scales[32 * q : 32 * q + 4, :, :].bitcast(I32),
+                in_=dest_scales[:, 4 * q : 4 * q + 4, :].rearrange("c r n -> r c n").bitcast(I32),
+            )
+        load_b(1, 0)
+        load_b(1, 1)
+        load_b(2, 0)
+        load_b(2, 1)
+        load_a(1)
+        load_b(3, 0)
+        load_b(3, 1)
+        nc.sync.dma_start(out=recept_in[:], in_=receptivity.rearrange("(G p t) -> p G t", G=2, t=4))
+        nc.sync.dma_start(out=outside_all[:], in_=outside.partition_broadcast(P))
+
+        def copy(eng, out, in_):
+            if eng == "V":
+                nc.vector.tensor_copy(out=out, in_=in_)
+            else:
+                nc.scalar.copy(out=out, in_=in_)
+
+        def new_grouped(key):
+            grouped[key] = turn.tile([P, W, 4], BF16, name="grouped", tag="grouped", bufs=7, align_bytes=64)
+            return grouped[key]
+
+        def interleave(eng, dst, src):
+            copy(eng, dst.rearrange("p (c i) t -> p c t i", i=4), src.rearrange("p t (c i) -> p c t i", i=4))
+
+        def quantize(key, cols=slice(0, W)):
+            nc.vector.quantize_mx(
+                out=codes[key][:, cols].bitcast(FP8X4),
+                scales=scales[key][:, cols],
+                in_=grouped[key][:, cols, :].rearrange("p w j -> p (w j)"),
+            )
+
+        def vperm():
+            nc.vector.tensor_copy(out=rows_perm[:].rearrange("p t (q i) -> p t q i", i=4),
+                                  in_=rows_in[:].rearrange("p (q t i) -> p t q i", t=4, i=4))
+
+        def vtr():
+            bank["vec"] = psum.tile([P, 4, P], BF16, name="vec_ps", tag="acc0")
+            for t in range(4):
+                nc.tensor.transpose(bank["vec"][:, t, :], rows_perm[:, t, :], ident[:])
+
+        def vch1():
+            nc.vector.tensor_copy(out=vec[:].rearrange("p v (t g) -> p v t g", g=4),
+                                  in_=bank["vec"][:, :, 0:12].rearrange("p t (v g) -> p v t g", g=4))
+            nc.vector.tensor_scalar(out=mant[:], in0=vec[:, 0, :].bitcast(I32), scalar1=0x007FFFFF, scalar2=0x3F800000,
+                                    op0=ALU.bitwise_and, op1=ALU.bitwise_or)
+
+        def vch3():
+            nc.vector.tensor_scalar(out=twice_pos[:], in0=vec[:, 0, :], scalar1=0.0, scalar2=2.0, op0=ALU.is_ge, op1=ALU.mult)
+            nc.vector.tensor_scalar(out=expo[:], in0=vec[:, 0, :].bitcast(I32), scalar1=23, scalar2=0xFF,
+                                    op0=ALU.logical_shift_right, op1=ALU.bitwise_and)
+            for v in range(2):
+                nc.vector.scalar_tensor_tensor(out=signed[:, v, :], in0=twice_pos[:], scalar=-1.0, in1=vec[:, 1 + v, :],
+                                               op0=ALU.add, op1=ALU.mult)
+            nc.vector.tensor_scalar(out=ln_pow[:], in0=expo[:], scalar1=-127.0, scalar2=LN2, op0=ALU.add, op1=ALU.mult)
+            nc.vector.tensor_scalar(out=ln_zero[:], in0=vec[:, 0, :], scalar1=0.0, scalar2=-1.0e4, op0=ALU.is_equal, op1=ALU.mult)
+
+        def ln():
+            nc.scalar.activation(out=ln_mant[:], in_=mant[:].bitcast(F32), func=ACT.Ln)
+
+        def vch2():
+            nc.vector.tensor_tensor(out=ln_base[:], in0=ln_pow[:], in1=ln_zero[:], op=ALU.add)
+            nc.vector.tensor_tensor(out=ln_mass[:], in0=ln_base[:], in1=ln_mant[:], op=ALU.add)
+
+        def lps():
+            nc.vector.tensor_copy(out=l_scales[:].bitcast(I32).rearrange("p (g t q) -> p g t q", g=4, t=4),
+                                  in_=l_scales_in[:].bitcast(I32).rearrange("p (g q t) -> p g t q", g=4, t=4))
+
+        def lpw():
+            nc.vector.tensor_copy(out=l_words[:].bitcast(I32).rearrange("p (g t q w) -> p g t q w", g=4, t=4, w=2),
+                                  in_=l_words_in[:].bitcast(I32).rearrange("p (g q t w) -> p g t q w", g=4, t=4, w=2))
+
+        def iz(eng):
+            interleave(eng, new_grouped("z")[:], z_rows[:])
+
+        def ib(g, c, eng):
+            dst = new_grouped(("b", g, c))
+            copy(eng, dst[:].rearrange("p (t q i) j -> p t q j i", t=4, i=4),
+                 b_rows[g, c][:].rearrange("p j (q t i) -> p t q j i", t=4, i=4))
+
+        def mp(g):
+            for t in range(4):
+                ps = psum.tile([P, W], F32, name="first", tag="first%d" % t)
+                bank["p", g, t] = ps
+                n = 4 * g + t
+                nc.tensor.matmul_mx(out=ps[:], lhsT=l_words[:, 2 * P * n : 2 * P * (n + 1)].bitcast(FP4X4),
+                                    lhsT_scale=l_scales[:, P * n : P * (n + 1)],
+                                    rhs=codes["z"][:].bitcast(FP8X4), rhs_scale=scales["z"][:], start=True, stop=True)
+
+        def new_evac(key):
+            evac[key] = turn.tile([P, 4, W], BF16, name="evac", tag="evac", bufs=7, align_bytes=64)
+            return evac[key]
+
+        def ep(g, eng):
+            dst = new_evac(("p", g))
+            for t in range(4):
+                n = 4 * t + g
+                nc.scalar.activation(out=dst[:, t, :], in_=bank["p", g, t][:], func=ACT.Identity,
+                                     scale=signed[:, 0, n : n + 1], bias=signed[:, 1, n : n + 1])
+
+        def mf(g, G):
+            for t in range(4):
+                ps = psum.tile([P, W], F32, name="first", tag="first%d" % t)
+                bank["f", g, G, t] = ps
+                for c in range(2):
+                    nc.tensor.matmul_mx(out=ps[:], lhsT=codes["b", g, c][:, P * t : P * (t + 1)].bitcast(FP8X4),
+                                        lhsT_scale=scales["b", g, c][:, P * t : P * (t + 1)],
+                                        rhs=a_words[G][:, c, :].bitcast(FP8X4),
+                                        rhs_scale=a_scales[:, c, G * W : (G + 1) * W], start=(c == 0), stop=(c == 1))
+
+        def ef(g, G):
+            dst = new_evac(("f", g, G))
+            for t in range(4):
+                n = 4 * t + g
+                nc.scalar.activation(out=dst[:, t, :].rearrange("p (u m) -> p u m", u=4),
+                                     in_=bank["f", g, G, t][:].rearrange("p (m u) -> p u m", u=4),
+                                     func=ACT.Exp, bias=ln_mass[:, n : n + 1])
+
+        def my(g, G):
+            for u in range(4):
+                if g == 0:
+                    bank["y", G, u] = psum.tile([P, S], F32, name="acc", tag="acc%d" % u)
+                nc.tensor.matmul_mx(out=bank["y", G, u][:], lhsT=codes["f", g, G][:, P * u : P * (u + 1)].bitcast(FP8X4),
+                                    lhsT_scale=scales["f", g, G][:, P * u : P * (u + 1)],
+                                    rhs=codes["p", g][:].bitcast(FP8X4), rhs_scale=scales["p", g][:],
+                                    start=(g == 0), stop=(g == 3))
+
+        def make_offset(G, eng):
+            if G == 0:
+                nc.vector.tensor_copy(out=recept[:], in_=recept_in[:])
+            for u in range(4):
+                if eng == "V":
+                    nc.vector.tensor_scalar(out=offset[:, G, u, :], in0=outside_all[:], scalar1=recept[:, G, u : u + 1],
+                                            scalar2=None, op0=ALU.mult)
+                else:
+                    nc.scalar.activation(out=offset[:, G, u, :], in_=outside_all[:], func=ACT.Copy,
+                                         scale=recept[:, G, u : u + 1])
+
+        def st(G, h, eng):
+            for u in (2 * h, 2 * h + 1):
+                nc.vector.scalar_tensor_tensor(out=y[G][:, u, :], in0=bank["y", G, u][:], scalar=recept[:, G, u : u + 1],
+                                               in1=offset[:, G, u, :], op0=ALU.mult, op1=ALU.add)
+            nc.sync.dma_start(
+                out=out_0[G * W : (G + 1) * W, :].rearrange("(p u) s -> p u s", u=4)[:, 2 * h : 2 * h + 2, :],
+                in_=y[G][:, 2 * h : 2 * h + 2, :],
+            )
+
+        def iy(G, h, eng):
+            if ("y", G) not in grouped:
+                new_grouped(("y", G))
+            cols = slice(h * 256, (h + 1) * 256)
+            interleave(eng, grouped["y", G][:, cols, :], y[G][:, :, cols])
+
+        done = set()
+
+        def qy(G, h):
+            cols = slice(h * 256, (h + 1) * 256)
+            quantize(("y", G), cols)
+            nc.sync.dma_start(
+                out=out_1[G].rearrange("p m t -> p (m t)")[:, h * 1024 : (h + 1) * 1024].bitcast(I32),
+                in_=codes["y", G][:, cols].bitcast(I32),
+            )
+            if (G, 1 - h) in done:
+                for q in range(4):
+                    nc.sync.dma_start(out=out_2[G, 4 * q : 4 * q + 4, :].bitcast(I32),
+                                      in_=scales["y", G][32 * q : 32 * q + 4, :].bitcast(I32))
+            done.add((G, h))
+
+        steps = {
+            "vperm": vperm, "vtr": vtr, "vch1": vch1, "vch3": vch3, "ln": ln, "vch2": vch2, "LPs": lps, "LPw": lpw,
+            "IZ": iz, "QZ": lambda: quantize("z"), "IB": ib, "QB": lambda g, c: quantize(("b", g, c)),
+            "mP": mp, "eP": ep, "IP": lambda g, eng: interleave(eng, new_grouped(("p", g))[:], evac["p", g][:]),
+            "QP": lambda g: quantize(("p", g)), "mF": mf, "eF": ef,
+            "IF": lambda g, G, eng: interleave(eng, new_grouped(("f", g, G))[:], evac["f", g, G][:]),
+            "QF": lambda g, G: quantize(("f", g, G)), "mY": my, "OR": make_offset, "st": st, "IY": iy, "QY": qy,
+        }
+        for step in SCHEDULE:
+            steps[step[0]](*step[1:])

@@ -20,7 +20,7 @@ P = 128
 W = 512
 LN2 = 0.6931471805599453
 
-SCHEDULE = [('IB', 0, 0, 'V'), ('vperm',), ('IZ', 'V'), ('vtr',), ('vch1',), ('QZ',), ('LPw',), ('LPs',), ('ln',), ('mP', 0), ('vch3',), ('QB', 0, 0), ('vch2',), ('IB', 0, 1, 'S'), ('QB', 0, 1), ('IB', 1, 0, 'V'), ('eP', 0, 'S'), ('IB', 1, 1, 'V'), ('mP', 1), ('eP', 1, 'S'), ('QB', 1, 0), ('QB', 1, 1), ('mF', 0, 0), ('IB', 2, 0, 'V'), ('eF', 0, 0), ('mF', 0, 1), ('IP', 0, 'V'), ('eF', 0, 1), ('mF', 1, 0), ('IP', 1, 'V'), ('IB', 3, 0, 'V'), ('eF', 1, 0), ('IB', 2, 1, 'V'), ('IF', 0, 0, 'V'), ('mP', 2), ('QB', 2, 1), ('QF', 0, 0), ('eP', 2, 'S'), ('QB', 2, 0), ('mF', 2, 0), ('IB', 3, 1, 'V'), ('QP', 0), ('mY', 0, 0), ('IF', 0, 1, 'V'), ('QP', 1), ('QB', 3, 1), ('eF', 2, 0), ('QB', 3, 0), ('mP', 3), ('OR', 0, 'V'), ('IP', 2, 'V'), ('eP', 3, 'S'), ('mF', 3, 0), ('eF', 3, 0), ('IP', 3, 'V'), ('IF', 1, 0, 'V'), ('mF', 1, 1), ('IF', 2, 0, 'V'), ('QF', 1, 0), ('eF', 1, 1), ('QF', 2, 0), ('mF', 2, 1), ('eF', 2, 1), ('QF', 0, 1), ('mY', 1, 0), ('IF', 3, 0, 'V'), ('QP', 2), ('IF', 2, 1, 'V'), ('QF', 3, 0), ('QP', 3), ('mF', 3, 1), ('IF', 1, 1, 'S'), ('mY', 2, 0), ('mY', 3, 0), ('eF', 3, 1), ('QF', 1, 1), ('st', 0, 0, 'V'), ('st', 0, 1, 'V'), ('IF', 3, 1, 'S'), ('mY', 0, 1), ('mY', 1, 1), ('QF', 2, 1), ('mY', 2, 1), ('OR', 1, 'S'), ('IY', 0, 0, 'V'), ('IY', 0, 1, 'V'), ('QF', 3, 1), ('QY', 0, 1), ('QY', 0, 0), ('mY', 3, 1), ('st', 1, 0, 'V'), ('st', 1, 1, 'V'), ('IY', 1, 1, 'V'), ('IY', 1, 0, 'S'), ('QY', 1, 1), ('QY', 1, 0)]
+SCHEDULE = [('vperm',), ('IB', 0, 0, 'S'), ('vtr',), ('IZ', 'V'), ('QZ',), ('vch1',), ('LPw',), ('LPs',), ('vch3',), ('QB', 0, 0), ('ln',), ('IB', 0, 1, 'V'), ('mP', 0), ('eP', 0, 'S'), ('mP', 1), ('vch2',), ('QB', 0, 1), ('IB', 1, 0, 'V'), ('eP', 1, 'S'), ('mF', 0, 0), ('IP', 0, 'V'), ('eF', 0, 0), ('QB', 1, 0), ('IP', 1, 'V'), ('IB', 1, 1, 'V'), ('IB', 2, 0, 'V'), ('QB', 1, 1), ('mF', 0, 1), ('QB', 2, 0), ('IB', 3, 0, 'V'), ('eF', 0, 1), ('mF', 1, 0), ('eF', 1, 0), ('mP', 2), ('IB', 2, 1, 'V'), ('IF', 0, 0, 'V'), ('QP', 0), ('QB', 2, 1), ('QF', 0, 0), ('eP', 2, 'S'), ('QP', 1), ('IB', 3, 1, 'V'), ('mF', 2, 0), ('IP', 2, 'V'), ('eF', 2, 0), ('mP', 3), ('OR', 0, 0, 'V'), ('QB', 3, 1), ('eP', 3, 'S'), ('QB', 3, 0), ('mY', 0, 0), ('mF', 3, 0), ('eF', 3, 0), ('IF', 0, 1, 'V'), ('IF', 2, 0, 'V'), ('QP', 2), ('IF', 1, 0, 'V'), ('IP', 3, 'V'), ('QF', 1, 0), ('mF', 1, 1), ('eF', 1, 1), ('IF', 3, 0, 'V'), ('QP', 3), ('mF', 2, 1), ('eF', 2, 1), ('mY', 1, 0), ('QF', 2, 0), ('mY', 2, 0), ('QF', 3, 0), ('OR', 0, 1, 'S'), ('QF', 0, 1), ('mY', 3, 0), ('IF', 1, 1, 'V'), ('st', 0, 0, 'V'), ('QF', 1, 1), ('mF', 3, 1), ('st', 0, 1, 'V'), ('IF', 2, 1, 'S'), ('mY', 0, 1), ('eF', 3, 1), ('QF', 2, 1), ('IY', 0, 0, 'S'), ('mY', 1, 1), ('IF', 3, 1, 'V'), ('mY', 2, 1), ('QF', 3, 1), ('OR', 1, 0, 'S'), ('mY', 3, 1), ('QY', 0, 0), ('st', 1, 0, 'V'), ('OR', 1, 1, 'S'), ('st', 1, 1, 'V'), ('IY', 1, 0, 'V'), ('IY', 0, 1, 'S'), ('QY', 0, 1), ('QY', 1, 0), ('IY', 1, 1, 'S'), ('QY', 1, 1)]
 
 
 def tile_gravity_mobility_importation_k4_kernel(
@@ -47,7 +47,6 @@ def tile_gravity_mobility_importation_k4_kernel(
         signed = kept("signed", [P, 2, 16], F32)
         ln_pow = kept("ln_pow", [P, 16], F32)
         ln_zero = kept("ln_zero", [P, 16], F32)
-        ln_base = kept("ln_base", [P, 16], F32)
         ln_mant = kept("ln_mant", [P, 16], F32)
         ln_mass = kept("ln_mass", [P, 16], F32)
         recept_in = kept("recept_in", [P, 2, 4], BF16)
@@ -61,7 +60,10 @@ def tile_gravity_mobility_importation_k4_kernel(
         a_words = [kept("a_words%d" % G, [P, 2, W], U32) for G in range(2)]
         a_scales = kept("a_scales", [P, 2, D], U8)
         z_rows = kept("z_rows", [P, 4, S], BF16)
-        b_rows = {(g, c): kept("b_rows%d%d" % (g, c), [P, 4, W], BF16) for g in range(4) for c in range(2)}
+        b_rows = {(g, c): kept("b_rows%d%d" % (g, c), [P, 4, W], BF16) for g in range(2) for c in range(2)}
+        b_pair = [kept("b_pair%d" % c, [P, 4, 2 * W], BF16) for c in range(2)]
+        warm = kept("warm", [P, 1], F32)
+        warm_out = kept("warm_out", [P, 1], F32)
         y = [kept("y%d" % G, [P, 4, S], F32) for G in range(2)]
         codes = {}
         scales = {}
@@ -74,15 +76,25 @@ def tile_gravity_mobility_importation_k4_kernel(
         evac = {}
         bank = {}
 
-        nc.vector.memset(rows_in[:].bitcast(I32), 0)
+        nc.gpsimd.memset(rows_in[:].bitcast(I32), 0)
+        nc.gpsimd.memset(warm[:], 1.0)
         nc.vector.memset(l_scales_in[:].bitcast(I32), 0)
-        nc.gpsimd.memset(a_scales[:].bitcast(I32), 0)
         make_identity(nc, ident[:])
+        nc.gpsimd.memset(a_scales[:].bitcast(I32), 0)
+        for v, vector_in in enumerate((mass, amplitude, common)):
+            nc.scalar.dma_start(out=rows_in[4 * v : 4 * v + 4, :], in_=vector_in.rearrange("(g x) -> g x", g=4))
+        nc.scalar.activation(out=warm_out[:], in_=warm[:], func=ACT.Ln)
 
         def load_b(g, c):
             nc.sync.dma_start(
                 out=b_rows[g, c][:],
                 in_=origin_feat[c * W : (c + 1) * W, g * W : (g + 1) * W].rearrange("(p j) o -> p j o", j=4),
+            )
+
+        def load_b_pair(c):
+            nc.sync.dma_start(
+                out=b_pair[c][:],
+                in_=origin_feat[c * W : (c + 1) * W, 2 * W : 4 * W].rearrange("(p j) o -> p j o", j=4),
             )
 
         def load_a(G):
@@ -91,17 +103,15 @@ def tile_gravity_mobility_importation_k4_kernel(
                 in_=dest_words.rearrange("c p n t -> p c (n t)")[:, :, G * 4 * W : (G + 1) * 4 * W].bitcast(I32),
             )
 
-        load_b(0, 0)
-        for v, vector_in in enumerate((mass, amplitude, common)):
-            nc.sync.dma_start(out=rows_in[4 * v : 4 * v + 4, :], in_=vector_in.rearrange("(g x) -> g x", g=4))
         nc.sync.dma_start(out=z_rows[:], in_=drivers.rearrange("(p j) s -> p j s", j=4))
-        load_b(0, 1)
+        load_b(0, 0)
         nc.sync.dma_start(out=l_words_in[:].bitcast(I32), in_=load_words[0].bitcast(I32))
         for q in range(4):
             nc.sync.dma_start(
                 out=l_scales_in[32 * q : 32 * q + 4, :].bitcast(I32),
                 in_=load_scales[0, 4 * q : 4 * q + 4, :].bitcast(I32),
             )
+        load_b(0, 1)
         load_a(0)
         for q in range(4):
             nc.sync.dma_start(
@@ -110,11 +120,9 @@ def tile_gravity_mobility_importation_k4_kernel(
             )
         load_b(1, 0)
         load_b(1, 1)
-        load_b(2, 0)
-        load_b(2, 1)
         load_a(1)
-        load_b(3, 0)
-        load_b(3, 1)
+        load_b_pair(0)
+        load_b_pair(1)
         nc.sync.dma_start(out=recept_in[:], in_=receptivity.rearrange("(G p t) -> p G t", G=2, t=4))
         nc.sync.dma_start(out=outside_all[:], in_=outside.partition_broadcast(P))
 
@@ -157,18 +165,17 @@ def tile_gravity_mobility_importation_k4_kernel(
             nc.vector.tensor_scalar(out=twice_pos[:], in0=vec[:, 0, :], scalar1=0.0, scalar2=2.0, op0=ALU.is_ge, op1=ALU.mult)
             nc.vector.tensor_scalar(out=expo[:], in0=vec[:, 0, :].bitcast(I32), scalar1=23, scalar2=0xFF,
                                     op0=ALU.logical_shift_right, op1=ALU.bitwise_and)
+            nc.vector.tensor_scalar(out=ln_zero[:], in0=vec[:, 0, :], scalar1=0.0, scalar2=-1.0e4, op0=ALU.is_equal, op1=ALU.mult)
             for v in range(2):
                 nc.vector.scalar_tensor_tensor(out=signed[:, v, :], in0=twice_pos[:], scalar=-1.0, in1=vec[:, 1 + v, :],
                                                op0=ALU.add, op1=ALU.mult)
-            nc.vector.tensor_scalar(out=ln_pow[:], in0=expo[:], scalar1=-127.0, scalar2=LN2, op0=ALU.add, op1=ALU.mult)
-            nc.vector.tensor_scalar(out=ln_zero[:], in0=vec[:, 0, :], scalar1=0.0, scalar2=-1.0e4, op0=ALU.is_equal, op1=ALU.mult)
+            nc.vector.scalar_tensor_tensor(out=ln_pow[:], in0=expo[:], scalar=-127.0, in1=ln_zero[:], op0=ALU.add, op1=ALU.add)
 
         def ln():
             nc.scalar.activation(out=ln_mant[:], in_=mant[:].bitcast(F32), func=ACT.Ln)
 
         def vch2():
-            nc.vector.tensor_tensor(out=ln_base[:], in0=ln_pow[:], in1=ln_zero[:], op=ALU.add)
-            nc.vector.tensor_tensor(out=ln_mass[:], in0=ln_base[:], in1=ln_mant[:], op=ALU.add)
+            nc.vector.scalar_tensor_tensor(out=ln_mass[:], in0=ln_pow[:], scalar=LN2, in1=ln_mant[:], op0=ALU.mult, op1=ALU.add)
 
         def lps():
             nc.vector.tensor_copy(out=l_scales[:].bitcast(I32).rearrange("p (g t q) -> p g t q", g=4, t=4),
@@ -184,7 +191,7 @@ def tile_gravity_mobility_importation_k4_kernel(
         def ib(g, c, eng):
             dst = new_grouped(("b", g, c))
             copy(eng, dst[:].rearrange("p (t q i) j -> p t q j i", t=4, i=4),
-                 b_rows[g, c][:].rearrange("p j (q t i) -> p t q j i", t=4, i=4))
+                 (b_rows[g, c][:] if g < 2 else b_pair[c][:, :, (g - 2) * W : (g - 1) * W]).rearrange("p j (q t i) -> p t q j i", t=4, i=4))
 
         def mp(g):
             for t in range(4):
@@ -233,10 +240,10 @@ def tile_gravity_mobility_importation_k4_kernel(
                                     rhs=codes["p", g][:].bitcast(FP8X4), rhs_scale=scales["p", g][:],
                                     start=(g == 0), stop=(g == 3))
 
-        def make_offset(G, eng):
-            if G == 0:
+        def make_offset(G, h, eng):
+            if G == 0 and h == 0:
                 nc.vector.tensor_copy(out=recept[:], in_=recept_in[:])
-            for u in range(4):
+            for u in (2 * h, 2 * h + 1):
                 if eng == "V":
                     nc.vector.tensor_scalar(out=offset[:, G, u, :], in0=outside_all[:], scalar1=recept[:, G, u : u + 1],
                                             scalar2=None, op0=ALU.mult)

@@ -18,9 +18,21 @@ ALU = mybir.AluOpType
 
 P = 128
 W = 512
+SLOTS = 4
+ORIGIN_GROUPS = O // W
+DEST_GROUPS = D // W
+FEATURE_GROUPS = K // W
+VECTOR_ROWS = 3 * ORIGIN_GROUPS
+WORD_BUFS = 7
+SLOT_BUFS = 10
 LN2 = 0.6931471805599453
+ZERO_MASS_EXPONENT = -1.0e4
 
-SCHEDULE = [('vperm',), ('IB', 0, 0, 'S'), ('vtr',), ('IZ', 'V'), ('QZ',), ('vch1',), ('LPw',), ('LPs',), ('vch3',), ('QB', 0, 0), ('ln',), ('IB', 0, 1, 'V'), ('mP', 0), ('eP', 0, 'S'), ('mP', 1), ('vch2',), ('QB', 0, 1), ('IB', 1, 0, 'V'), ('eP', 1, 'S'), ('mF', 0, 0), ('IP', 0, 'V'), ('eF', 0, 0), ('QB', 1, 0), ('IP', 1, 'V'), ('IB', 1, 1, 'V'), ('IB', 2, 0, 'V'), ('QB', 1, 1), ('mF', 0, 1), ('QB', 2, 0), ('IB', 3, 0, 'V'), ('eF', 0, 1), ('mF', 1, 0), ('eF', 1, 0), ('mP', 2), ('IB', 2, 1, 'V'), ('IF', 0, 0, 'V'), ('QP', 0), ('QB', 2, 1), ('QF', 0, 0), ('eP', 2, 'S'), ('QP', 1), ('IB', 3, 1, 'V'), ('mF', 2, 0), ('IP', 2, 'V'), ('eF', 2, 0), ('mP', 3), ('OR', 0, 0, 'V'), ('QB', 3, 1), ('eP', 3, 'S'), ('QB', 3, 0), ('mY', 0, 0), ('mF', 3, 0), ('eF', 3, 0), ('IF', 0, 1, 'V'), ('IF', 2, 0, 'V'), ('QP', 2), ('IF', 1, 0, 'V'), ('IP', 3, 'V'), ('QF', 1, 0), ('mF', 1, 1), ('eF', 1, 1), ('IF', 3, 0, 'V'), ('QP', 3), ('mF', 2, 1), ('eF', 2, 1), ('mY', 1, 0), ('QF', 2, 0), ('mY', 2, 0), ('QF', 3, 0), ('OR', 0, 1, 'S'), ('QF', 0, 1), ('mY', 3, 0), ('IF', 1, 1, 'V'), ('st', 0, 0, 'V'), ('QF', 1, 1), ('mF', 3, 1), ('st', 0, 1, 'V'), ('IF', 2, 1, 'S'), ('mY', 0, 1), ('eF', 3, 1), ('QF', 2, 1), ('IY', 0, 0, 'S'), ('mY', 1, 1), ('IF', 3, 1, 'V'), ('mY', 2, 1), ('QF', 3, 1), ('OR', 1, 0, 'S'), ('mY', 3, 1), ('QY', 0, 0), ('st', 1, 0, 'V'), ('OR', 1, 1, 'S'), ('st', 1, 1, 'V'), ('IY', 1, 0, 'V'), ('IY', 0, 1, 'S'), ('QY', 0, 1), ('QY', 1, 0), ('IY', 1, 1, 'S'), ('QY', 1, 1)]
+WHOLE = slice(0, W)
+FIRST_HALF = slice(0, W // 2)
+SECOND_HALF = slice(W // 2, W)
+VECTOR_SHARE = slice(0, 3 * W // 4)
+SCALAR_SHARE = slice(3 * W // 4, W)
 
 
 def tile_gravity_mobility_importation_k4_kernel(
@@ -30,264 +42,333 @@ def tile_gravity_mobility_importation_k4_kernel(
     nc = tc.nc
     with ExitStack() as ctx:
         keep = ctx.enter_context(tc.tile_pool(name="keep", bufs=1))
-        turn = ctx.enter_context(tc.tile_pool(name="turn", bufs=1))
+        staging = ctx.enter_context(tc.tile_pool(name="staging", bufs=1))
         psum = ctx.enter_context(tc.psum_pool(name="psum", bufs=1))
         ctx.enter_context(tc.manual_schedule())
 
         def kept(name, shape, dtype):
             return keep.tile(shape, dtype, name=name, align_bytes=64)
 
-        rows_in = kept("rows_in", [P, W], BF16)
-        rows_perm = kept("rows_perm", [P, 4, P], BF16)
+        vector_rows = kept("vector_rows", [VECTOR_ROWS, W], BF16)
+        vector_rows_by_slot = kept("vector_rows_by_slot", [P, SLOTS, P], BF16)
         ident = kept("ident", [P, P], BF16)
-        vec = kept("vec", [P, 3, 16], F32)
-        mant = kept("mant", [P, 16], I32)
-        expo = kept("expo", [P, 16], I32)
-        twice_pos = kept("twice_pos", [P, 16], F32)
+        per_origin = kept("per_origin", [P, 3, 16], F32)
+        mantissa = kept("mantissa", [P, 16], I32)
+        exponent_bits = kept("exponent_bits", [P, 16], I32)
+        twice_nonneg = kept("twice_nonneg", [P, 16], F32)
         signed = kept("signed", [P, 2, 16], F32)
-        ln_pow = kept("ln_pow", [P, 16], F32)
-        ln_zero = kept("ln_zero", [P, 16], F32)
-        ln_mant = kept("ln_mant", [P, 16], F32)
+        exponent = kept("exponent", [P, 16], F32)
+        zero_shift = kept("zero_shift", [P, 16], F32)
+        ln_mantissa = kept("ln_mantissa", [P, 16], F32)
         ln_mass = kept("ln_mass", [P, 16], F32)
-        recept_in = kept("recept_in", [P, 2, 4], BF16)
-        recept = kept("recept", [P, 2, 4], F32)
+        recept_in = kept("recept_in", [P, DEST_GROUPS, SLOTS], BF16)
+        recept = kept("recept", [P, DEST_GROUPS, SLOTS], F32)
         outside_all = kept("outside_all", [P, S], BF16)
-        offset = kept("offset", [P, 2, 4, S], F32)
+        offset = kept("offset", [P, DEST_GROUPS, SLOTS, S], F32)
         l_words_in = kept("l_words_in", [P, 2 * O], U8)
         l_words = kept("l_words", [P, 2 * O], U8)
         l_scales_in = kept("l_scales_in", [P, O], U8)
         l_scales = kept("l_scales", [P, O], U8)
-        a_words = [kept("a_words%d" % G, [P, 2, W], U32) for G in range(2)]
-        a_scales = kept("a_scales", [P, 2, D], U8)
-        z_rows = kept("z_rows", [P, 4, S], BF16)
-        b_rows = {(g, c): kept("b_rows%d%d" % (g, c), [P, 4, W], BF16) for g in range(2) for c in range(2)}
-        b_pair = [kept("b_pair%d" % c, [P, 4, 2 * W], BF16) for c in range(2)]
+        a_words = [kept("a_words%d" % d, [P, FEATURE_GROUPS, W], U32) for d in range(DEST_GROUPS)]
+        a_scales = kept("a_scales", [P, FEATURE_GROUPS, D], U8)
+        z_rows = kept("z_rows", [P, SLOTS, S], BF16)
+        b_early = {(g, c): kept("b_early%d%d" % (g, c), [P, SLOTS, W], BF16) for g in range(2) for c in range(FEATURE_GROUPS)}
+        b_late = [kept("b_late%d" % c, [P, SLOTS, 2 * W], BF16) for c in range(FEATURE_GROUPS)]
         warm = kept("warm", [P, 1], F32)
-        warm_out = kept("warm_out", [P, 1], F32)
-        y = [kept("y%d" % G, [P, 4, S], F32) for G in range(2)]
-        codes = {}
-        scales = {}
-        for key in (["z"] + [("b", g, c) for g in range(4) for c in range(2)] + [("p", g) for g in range(4)]
-                    + [("f", g, G) for g in range(4) for G in range(2)] + [("y", G) for G in range(2)]):
-            label = "".join(str(x) for x in key)
-            codes[key] = kept("codes_" + label, [P, W], U32)
-            scales[key] = kept("scales_" + label, [P, W], U8)
-        grouped = {}
-        evac = {}
+        warm_ln = kept("warm_ln", [P, 1], F32)
+        warm_exp = kept("warm_exp", [P, 1], F32)
+        y = [kept("y%d" % d, [P, SLOTS, S], F32) for d in range(DEST_GROUPS)]
+
+        keys = [("z",)]
+        keys += [("b", g, c) for g in range(ORIGIN_GROUPS) for c in range(FEATURE_GROUPS)]
+        keys += [("prev", g) for g in range(ORIGIN_GROUPS)]
+        keys += [("flow", g, d) for g in range(ORIGIN_GROUPS) for d in range(DEST_GROUPS)]
+        keys += [("y", d) for d in range(DEST_GROUPS)]
+        codes = {key: kept("codes_" + "".join(map(str, key)), [P, W], U32) for key in keys}
+        scales = {key: kept("scales_" + "".join(map(str, key)), [P, W], U8) for key in keys}
+        by_slot = {("z",): z_rows, ("y", 0): y[0], ("y", 1): y[1]}
+        by_word = {}
         bank = {}
 
-        nc.gpsimd.memset(rows_in[:].bitcast(I32), 0)
+        nc.gpsimd.memset(vector_rows_by_slot[:].rearrange("p t m -> p (t m)").bitcast(I32), 0)
         nc.gpsimd.memset(warm[:], 1.0)
         nc.vector.memset(l_scales_in[:].bitcast(I32), 0)
         make_identity(nc, ident[:])
         nc.gpsimd.memset(a_scales[:].bitcast(I32), 0)
-        for v, vector_in in enumerate((mass, amplitude, common)):
-            nc.scalar.dma_start(out=rows_in[4 * v : 4 * v + 4, :], in_=vector_in.rearrange("(g x) -> g x", g=4))
-        nc.scalar.activation(out=warm_out[:], in_=warm[:], func=ACT.Ln)
+        nc.scalar.activation(out=warm_ln[:], in_=warm[:], func=ACT.Ln)
 
-        def load_b(g, c):
+        def load_b(tile, c, origins):
+            nc.sync.dma_start(out=tile[:], in_=origin_feat[c * W : (c + 1) * W, origins].rearrange("(p j) o -> p j o", j=SLOTS))
+
+        def load_a(d):
             nc.sync.dma_start(
-                out=b_rows[g, c][:],
-                in_=origin_feat[c * W : (c + 1) * W, g * W : (g + 1) * W].rearrange("(p j) o -> p j o", j=4),
+                out=a_words[d][:].bitcast(I32),
+                in_=dest_words.rearrange("c p n j -> p c (n j)")[:, :, d * SLOTS * W : (d + 1) * SLOTS * W].bitcast(I32),
             )
 
-        def load_b_pair(c):
-            nc.sync.dma_start(
-                out=b_pair[c][:],
-                in_=origin_feat[c * W : (c + 1) * W, 2 * W : 4 * W].rearrange("(p j) o -> p j o", j=4),
-            )
-
-        def load_a(G):
-            nc.sync.dma_start(
-                out=a_words[G][:].bitcast(I32),
-                in_=dest_words.rearrange("c p n t -> p c (n t)")[:, :, G * 4 * W : (G + 1) * 4 * W].bitcast(I32),
-            )
-
-        nc.sync.dma_start(out=z_rows[:], in_=drivers.rearrange("(p j) s -> p j s", j=4))
-        load_b(0, 0)
+        for v, source in enumerate((mass, amplitude, common)):
+            nc.sync.dma_start(out=vector_rows[ORIGIN_GROUPS * v : ORIGIN_GROUPS * (v + 1), :],
+                              in_=source.rearrange("(g x) -> g x", g=ORIGIN_GROUPS))
+        nc.sync.dma_start(out=z_rows[:], in_=drivers.rearrange("(p j) s -> p j s", j=SLOTS))
+        load_b(b_early[0, 0], 0, slice(0, W))
         nc.sync.dma_start(out=l_words_in[:].bitcast(I32), in_=load_words[0].bitcast(I32))
-        for q in range(4):
-            nc.sync.dma_start(
-                out=l_scales_in[32 * q : 32 * q + 4, :].bitcast(I32),
-                in_=load_scales[0, 4 * q : 4 * q + 4, :].bitcast(I32),
-            )
-        load_b(0, 1)
+        for quad in range(4):
+            nc.sync.dma_start(out=l_scales_in[32 * quad : 32 * quad + 4, :].bitcast(I32),
+                              in_=load_scales[0, 4 * quad : 4 * quad + 4, :].bitcast(I32))
+        load_b(b_early[0, 1], 1, slice(0, W))
         load_a(0)
-        for q in range(4):
-            nc.sync.dma_start(
-                out=a_scales[32 * q : 32 * q + 4, :, :].bitcast(I32),
-                in_=dest_scales[:, 4 * q : 4 * q + 4, :].rearrange("c r n -> r c n").bitcast(I32),
-            )
-        load_b(1, 0)
-        load_b(1, 1)
+        for quad in range(4):
+            nc.sync.dma_start(out=a_scales[32 * quad : 32 * quad + 4, :, :].bitcast(I32),
+                              in_=dest_scales[:, 4 * quad : 4 * quad + 4, :].rearrange("c r n -> r c n").bitcast(I32))
+        load_b(b_early[1, 0], 0, slice(W, 2 * W))
+        load_b(b_early[1, 1], 1, slice(W, 2 * W))
         load_a(1)
-        load_b_pair(0)
-        load_b_pair(1)
-        nc.sync.dma_start(out=recept_in[:], in_=receptivity.rearrange("(G p t) -> p G t", G=2, t=4))
+        load_b(b_late[0], 0, slice(2 * W, O))
+        load_b(b_late[1], 1, slice(2 * W, O))
+        nc.sync.dma_start(out=recept_in[:], in_=receptivity.rearrange("(d p u) -> p d u", d=DEST_GROUPS, u=SLOTS))
         nc.sync.dma_start(out=outside_all[:], in_=outside.partition_broadcast(P))
 
-        def copy(eng, out, in_):
-            if eng == "V":
-                nc.vector.tensor_copy(out=out, in_=in_)
-            else:
-                nc.scalar.copy(out=out, in_=in_)
+        def on_vector(out, in_):
+            nc.vector.tensor_copy(out=out, in_=in_)
 
-        def new_grouped(key):
-            grouped[key] = turn.tile([P, W, 4], BF16, name="grouped", tag="grouped", bufs=7, align_bytes=64)
-            return grouped[key]
+        def on_scalar(out, in_):
+            nc.scalar.copy(out=out, in_=in_)
 
-        def interleave(eng, dst, src):
-            copy(eng, dst.rearrange("p (c i) t -> p c t i", i=4), src.rearrange("p t (c i) -> p c t i", i=4))
+        def word_tile(key):
+            if key not in by_word:
+                by_word[key] = staging.tile([P, W, SLOTS], BF16, name="by_word", tag="by_word", bufs=WORD_BUFS, align_bytes=64)
+            return by_word[key]
 
-        def quantize(key, cols=slice(0, W)):
-            nc.vector.quantize_mx(
-                out=codes[key][:, cols].bitcast(FP8X4),
-                scales=scales[key][:, cols],
-                in_=grouped[key][:, cols, :].rearrange("p w j -> p (w j)"),
-            )
+        def slot_tile(key):
+            by_slot[key] = staging.tile([P, SLOTS, W], BF16, name="by_slot", tag="by_slot", bufs=SLOT_BUFS, align_bytes=64)
+            return by_slot[key]
 
-        def vperm():
-            nc.vector.tensor_copy(out=rows_perm[:].rearrange("p t (q i) -> p t q i", i=4),
-                                  in_=rows_in[:].rearrange("p (q t i) -> p t q i", t=4, i=4))
+        def interleave(copy, key, cols=WHOLE):
+            copy(word_tile(key)[:, cols, :].rearrange("p (n i) t -> p n t i", i=4),
+                 by_slot[key][:, :, cols].rearrange("p t (n i) -> p n t i", i=4))
 
-        def vtr():
-            bank["vec"] = psum.tile([P, 4, P], BF16, name="vec_ps", tag="acc0")
-            for t in range(4):
-                nc.tensor.transpose(bank["vec"][:, t, :], rows_perm[:, t, :], ident[:])
+        def interleave_b(copy, g, c, slots=slice(0, SLOTS)):
+            rows = b_early[g, c][:] if g < 2 else b_late[c][:, :, (g - 2) * W : (g - 1) * W]
+            copy(word_tile(("b", g, c))[:].rearrange("p (t q i) j -> p t q j i", t=SLOTS, i=4)[:, slots],
+                 rows.rearrange("p j (q t i) -> p t q j i", t=SLOTS, i=4)[:, slots])
 
-        def vch1():
-            nc.vector.tensor_copy(out=vec[:].rearrange("p v (t g) -> p v t g", g=4),
-                                  in_=bank["vec"][:, :, 0:12].rearrange("p t (v g) -> p v t g", g=4))
-            nc.vector.tensor_scalar(out=mant[:], in0=vec[:, 0, :].bitcast(I32), scalar1=0x007FFFFF, scalar2=0x3F800000,
-                                    op0=ALU.bitwise_and, op1=ALU.bitwise_or)
+        def quantize(key, cols=WHOLE):
+            nc.vector.quantize_mx(out=codes[key][:, cols].bitcast(FP8X4), scales=scales[key][:, cols],
+                                  in_=by_word[key][:, cols, :].rearrange("p n t -> p (n t)"))
 
-        def vch3():
-            nc.vector.tensor_scalar(out=twice_pos[:], in0=vec[:, 0, :], scalar1=0.0, scalar2=2.0, op0=ALU.is_ge, op1=ALU.mult)
-            nc.vector.tensor_scalar(out=expo[:], in0=vec[:, 0, :].bitcast(I32), scalar1=23, scalar2=0xFF,
+        def turn_vectors():
+            nc.vector.tensor_copy(out=vector_rows_by_slot[0:VECTOR_ROWS].rearrange("r t (q i) -> r t q i", i=4),
+                                  in_=vector_rows[:].rearrange("r (q t i) -> r t q i", t=SLOTS, i=4))
+            bank["vectors"] = psum.tile([P, SLOTS, P], BF16, name="vectors", tag="sum0")
+            for t in range(SLOTS):
+                nc.tensor.transpose(bank["vectors"][:, t, :], vector_rows_by_slot[:, t, :], ident[:])
+
+        def mass_mantissa():
+            nc.vector.tensor_copy(out=per_origin[:].rearrange("p v (t g) -> p v t g", g=ORIGIN_GROUPS),
+                                  in_=bank["vectors"][:, :, 0:VECTOR_ROWS].rearrange("p t (v g) -> p v t g", g=ORIGIN_GROUPS))
+            nc.vector.tensor_scalar(out=mantissa[:], in0=per_origin[:, 0, :].bitcast(I32), scalar1=0x007FFFFF,
+                                    scalar2=0x3F800000, op0=ALU.bitwise_and, op1=ALU.bitwise_or)
+            nc.scalar.activation(out=ln_mantissa[:], in_=mantissa[:].bitcast(F32), func=ACT.Ln)
+            nc.scalar.activation(out=warm_exp[:], in_=warm[:], func=ACT.Exp)
+
+        def mass_sign_and_exponent():
+            nc.vector.tensor_scalar(out=twice_nonneg[:], in0=per_origin[:, 0, :], scalar1=0.0, scalar2=2.0,
+                                    op0=ALU.is_ge, op1=ALU.mult)
+            nc.vector.tensor_scalar(out=exponent_bits[:], in0=per_origin[:, 0, :].bitcast(I32), scalar1=23, scalar2=0xFF,
                                     op0=ALU.logical_shift_right, op1=ALU.bitwise_and)
-            nc.vector.tensor_scalar(out=ln_zero[:], in0=vec[:, 0, :], scalar1=0.0, scalar2=-1.0e4, op0=ALU.is_equal, op1=ALU.mult)
+            nc.vector.tensor_scalar(out=zero_shift[:], in0=per_origin[:, 0, :], scalar1=0.0, scalar2=ZERO_MASS_EXPONENT,
+                                    op0=ALU.is_equal, op1=ALU.mult)
             for v in range(2):
-                nc.vector.scalar_tensor_tensor(out=signed[:, v, :], in0=twice_pos[:], scalar=-1.0, in1=vec[:, 1 + v, :],
-                                               op0=ALU.add, op1=ALU.mult)
-            nc.vector.scalar_tensor_tensor(out=ln_pow[:], in0=expo[:], scalar=-127.0, in1=ln_zero[:], op0=ALU.add, op1=ALU.add)
+                nc.vector.scalar_tensor_tensor(out=signed[:, v, :], in0=twice_nonneg[:], scalar=-1.0,
+                                               in1=per_origin[:, 1 + v, :], op0=ALU.add, op1=ALU.mult)
+            nc.vector.scalar_tensor_tensor(out=exponent[:], in0=exponent_bits[:], scalar=-127.0, in1=zero_shift[:],
+                                           op0=ALU.add, op1=ALU.add)
 
-        def ln():
-            nc.scalar.activation(out=ln_mant[:], in_=mant[:].bitcast(F32), func=ACT.Ln)
+        def mass_logarithm():
+            nc.vector.scalar_tensor_tensor(out=ln_mass[:], in0=exponent[:], scalar=LN2, in1=ln_mantissa[:],
+                                           op0=ALU.mult, op1=ALU.add)
 
-        def vch2():
-            nc.vector.scalar_tensor_tensor(out=ln_mass[:], in0=ln_pow[:], scalar=LN2, in1=ln_mant[:], op0=ALU.mult, op1=ALU.add)
+        def order_l_columns():
+            nc.vector.tensor_copy(
+                out=l_words[:].bitcast(I32).rearrange("p (g t q w) -> p g t q w", g=ORIGIN_GROUPS, t=SLOTS, w=2),
+                in_=l_words_in[:].bitcast(I32).rearrange("p (g q t w) -> p g t q w", g=ORIGIN_GROUPS, t=SLOTS, w=2))
+            nc.vector.tensor_copy(
+                out=l_scales[:].bitcast(I32).rearrange("p (g t q) -> p g t q", g=ORIGIN_GROUPS, t=SLOTS),
+                in_=l_scales_in[:].bitcast(I32).rearrange("p (g q t) -> p g t q", g=ORIGIN_GROUPS, t=SLOTS))
 
-        def lps():
-            nc.vector.tensor_copy(out=l_scales[:].bitcast(I32).rearrange("p (g t q) -> p g t q", g=4, t=4),
-                                  in_=l_scales_in[:].bitcast(I32).rearrange("p (g q t) -> p g t q", g=4, t=4))
+        def first_stage_bank(key, t):
+            bank[key, t] = psum.tile([P, W], F32, name="first", tag="first%d" % t)
+            return bank[key, t]
 
-        def lpw():
-            nc.vector.tensor_copy(out=l_words[:].bitcast(I32).rearrange("p (g t q w) -> p g t q w", g=4, t=4, w=2),
-                                  in_=l_words_in[:].bitcast(I32).rearrange("p (g q t w) -> p g t q w", g=4, t=4, w=2))
-
-        def iz(eng):
-            interleave(eng, new_grouped("z")[:], z_rows[:])
-
-        def ib(g, c, eng):
-            dst = new_grouped(("b", g, c))
-            copy(eng, dst[:].rearrange("p (t q i) j -> p t q j i", t=4, i=4),
-                 (b_rows[g, c][:] if g < 2 else b_pair[c][:, :, (g - 2) * W : (g - 1) * W]).rearrange("p j (q t i) -> p t q j i", t=4, i=4))
-
-        def mp(g):
-            for t in range(4):
-                ps = psum.tile([P, W], F32, name="first", tag="first%d" % t)
-                bank["p", g, t] = ps
-                n = 4 * g + t
-                nc.tensor.matmul_mx(out=ps[:], lhsT=l_words[:, 2 * P * n : 2 * P * (n + 1)].bitcast(FP4X4),
+        def multiply_prev(g):
+            for t in range(SLOTS):
+                n = SLOTS * g + t
+                nc.tensor.matmul_mx(out=first_stage_bank(("prev", g), t)[:],
+                                    lhsT=l_words[:, 2 * P * n : 2 * P * (n + 1)].bitcast(FP4X4),
                                     lhsT_scale=l_scales[:, P * n : P * (n + 1)],
-                                    rhs=codes["z"][:].bitcast(FP8X4), rhs_scale=scales["z"][:], start=True, stop=True)
+                                    rhs=codes["z",][:].bitcast(FP8X4), rhs_scale=scales["z",][:], start=True, stop=True)
 
-        def new_evac(key):
-            evac[key] = turn.tile([P, 4, W], BF16, name="evac", tag="evac", bufs=7, align_bytes=64)
-            return evac[key]
-
-        def ep(g, eng):
-            dst = new_evac(("p", g))
-            for t in range(4):
-                n = 4 * t + g
-                nc.scalar.activation(out=dst[:, t, :], in_=bank["p", g, t][:], func=ACT.Identity,
+        def empty_prev(g):
+            rows = slot_tile(("prev", g))
+            for t in range(SLOTS):
+                n = ORIGIN_GROUPS * t + g
+                nc.scalar.activation(out=rows[:, t, :], in_=bank[("prev", g), t][:], func=ACT.Identity,
                                      scale=signed[:, 0, n : n + 1], bias=signed[:, 1, n : n + 1])
 
-        def mf(g, G):
-            for t in range(4):
-                ps = psum.tile([P, W], F32, name="first", tag="first%d" % t)
-                bank["f", g, G, t] = ps
-                for c in range(2):
-                    nc.tensor.matmul_mx(out=ps[:], lhsT=codes["b", g, c][:, P * t : P * (t + 1)].bitcast(FP8X4),
+        def multiply_flow(g, d):
+            for t in range(SLOTS):
+                scores = first_stage_bank(("flow", g, d), t)
+                for c in range(FEATURE_GROUPS):
+                    nc.tensor.matmul_mx(out=scores[:], lhsT=codes["b", g, c][:, P * t : P * (t + 1)].bitcast(FP8X4),
                                         lhsT_scale=scales["b", g, c][:, P * t : P * (t + 1)],
-                                        rhs=a_words[G][:, c, :].bitcast(FP8X4),
-                                        rhs_scale=a_scales[:, c, G * W : (G + 1) * W], start=(c == 0), stop=(c == 1))
+                                        rhs=a_words[d][:, c, :].bitcast(FP8X4), rhs_scale=a_scales[:, c, d * W : (d + 1) * W],
+                                        start=(c == 0), stop=(c == FEATURE_GROUPS - 1))
 
-        def ef(g, G):
-            dst = new_evac(("f", g, G))
-            for t in range(4):
-                n = 4 * t + g
-                nc.scalar.activation(out=dst[:, t, :].rearrange("p (u m) -> p u m", u=4),
-                                     in_=bank["f", g, G, t][:].rearrange("p (m u) -> p u m", u=4),
+        def empty_flow(g, d):
+            rows = slot_tile(("flow", g, d))
+            for t in range(SLOTS):
+                n = ORIGIN_GROUPS * t + g
+                nc.scalar.activation(out=rows[:, t, :].rearrange("p (u m) -> p u m", u=SLOTS),
+                                     in_=bank[("flow", g, d), t][:].rearrange("p (m u) -> p u m", u=SLOTS),
                                      func=ACT.Exp, bias=ln_mass[:, n : n + 1])
 
-        def my(g, G):
-            for u in range(4):
+        def multiply_y(g, d):
+            for u in range(SLOTS):
                 if g == 0:
-                    bank["y", G, u] = psum.tile([P, S], F32, name="acc", tag="acc%d" % u)
-                nc.tensor.matmul_mx(out=bank["y", G, u][:], lhsT=codes["f", g, G][:, P * u : P * (u + 1)].bitcast(FP8X4),
-                                    lhsT_scale=scales["f", g, G][:, P * u : P * (u + 1)],
-                                    rhs=codes["p", g][:].bitcast(FP8X4), rhs_scale=scales["p", g][:],
-                                    start=(g == 0), stop=(g == 3))
+                    bank[("y", d), u] = psum.tile([P, S], F32, name="sum", tag="sum%d" % u)
+                nc.tensor.matmul_mx(out=bank[("y", d), u][:],
+                                    lhsT=codes["flow", g, d][:, P * u : P * (u + 1)].bitcast(FP8X4),
+                                    lhsT_scale=scales["flow", g, d][:, P * u : P * (u + 1)],
+                                    rhs=codes["prev", g][:].bitcast(FP8X4), rhs_scale=scales["prev", g][:],
+                                    start=(g == 0), stop=(g == ORIGIN_GROUPS - 1))
 
-        def make_offset(G, h, eng):
-            if G == 0 and h == 0:
-                nc.vector.tensor_copy(out=recept[:], in_=recept_in[:])
-            for u in (2 * h, 2 * h + 1):
-                if eng == "V":
-                    nc.vector.tensor_scalar(out=offset[:, G, u, :], in0=outside_all[:], scalar1=recept[:, G, u : u + 1],
-                                            scalar2=None, op0=ALU.mult)
-                else:
-                    nc.scalar.activation(out=offset[:, G, u, :], in_=outside_all[:], func=ACT.Copy,
-                                         scale=recept[:, G, u : u + 1])
+        def offset_on_vector(d, pair):
+            for u in (2 * pair, 2 * pair + 1):
+                nc.vector.tensor_scalar(out=offset[:, d, u, :], in0=outside_all[:], scalar1=recept[:, d, u : u + 1],
+                                        scalar2=None, op0=ALU.mult)
 
-        def st(G, h, eng):
-            for u in (2 * h, 2 * h + 1):
-                nc.vector.scalar_tensor_tensor(out=y[G][:, u, :], in0=bank["y", G, u][:], scalar=recept[:, G, u : u + 1],
-                                               in1=offset[:, G, u, :], op0=ALU.mult, op1=ALU.add)
+        def offset_on_scalar(d, pair):
+            for u in (2 * pair, 2 * pair + 1):
+                nc.scalar.activation(out=offset[:, d, u, :], in_=outside_all[:], func=ACT.Copy, scale=recept[:, d, u : u + 1])
+
+        def empty_y(d):
+            for pair in range(2):
+                for u in (2 * pair, 2 * pair + 1):
+                    nc.vector.scalar_tensor_tensor(out=y[d][:, u, :], in0=bank[("y", d), u][:], scalar=recept[:, d, u : u + 1],
+                                                   in1=offset[:, d, u, :], op0=ALU.mult, op1=ALU.add)
+                nc.sync.dma_start(
+                    out=out_0[d * W : (d + 1) * W, :].rearrange("(p u) s -> p u s", u=SLOTS)[:, 2 * pair : 2 * pair + 2, :],
+                    in_=y[d][:, 2 * pair : 2 * pair + 2, :])
+
+        def quantize_y(d, cols):
+            quantize(("y", d), cols)
             nc.sync.dma_start(
-                out=out_0[G * W : (G + 1) * W, :].rearrange("(p u) s -> p u s", u=4)[:, 2 * h : 2 * h + 2, :],
-                in_=y[G][:, 2 * h : 2 * h + 2, :],
-            )
+                out=out_1[d].rearrange("p s u -> p (s u)")[:, SLOTS * cols.start : SLOTS * cols.stop].bitcast(I32),
+                in_=codes["y", d][:, cols].bitcast(I32))
 
-        def iy(G, h, eng):
-            if ("y", G) not in grouped:
-                new_grouped(("y", G))
-            cols = slice(h * 256, (h + 1) * 256)
-            interleave(eng, grouped["y", G][:, cols, :], y[G][:, :, cols])
+        def store_y_scales(d, queues):
+            for quad in range(4):
+                queues[quad % len(queues)].dma_start(out=out_2[d, 4 * quad : 4 * quad + 4, :].bitcast(I32),
+                                                     in_=scales["y", d][32 * quad : 32 * quad + 4, :].bitcast(I32))
 
-        done = set()
 
-        def qy(G, h):
-            cols = slice(h * 256, (h + 1) * 256)
-            quantize(("y", G), cols)
-            nc.sync.dma_start(
-                out=out_1[G].rearrange("p m t -> p (m t)")[:, h * 1024 : (h + 1) * 1024].bitcast(I32),
-                in_=codes["y", G][:, cols].bitcast(I32),
-            )
-            if (G, 1 - h) in done:
-                for q in range(4):
-                    nc.sync.dma_start(out=out_2[G, 4 * q : 4 * q + 4, :].bitcast(I32),
-                                      in_=scales["y", G][32 * q : 32 * q + 4, :].bitcast(I32))
-            done.add((G, h))
+        turn_vectors()
+        interleave(on_scalar, ("z",), SECOND_HALF)
+        interleave(on_vector, ("z",), FIRST_HALF)
+        mass_mantissa()
+        mass_sign_and_exponent()
+        quantize(("z",))
+        interleave_b(on_scalar, 0, 0, slice(2, 4))
+        order_l_columns()
+        multiply_prev(0)
+        interleave_b(on_vector, 0, 0, slice(0, 2))
+        empty_prev(0)
+        interleave_b(on_vector, 0, 1)
+        quantize(("b", 0, 0))
+        mass_logarithm()
+        quantize(("b", 0, 1))
+        multiply_prev(1)
+        empty_prev(1)
 
-        steps = {
-            "vperm": vperm, "vtr": vtr, "vch1": vch1, "vch3": vch3, "ln": ln, "vch2": vch2, "LPs": lps, "LPw": lpw,
-            "IZ": iz, "QZ": lambda: quantize("z"), "IB": ib, "QB": lambda g, c: quantize(("b", g, c)),
-            "mP": mp, "eP": ep, "IP": lambda g, eng: interleave(eng, new_grouped(("p", g))[:], evac["p", g][:]),
-            "QP": lambda g: quantize(("p", g)), "mF": mf, "eF": ef,
-            "IF": lambda g, G, eng: interleave(eng, new_grouped(("f", g, G))[:], evac["f", g, G][:]),
-            "QF": lambda g, G: quantize(("f", g, G)), "mY": my, "OR": make_offset, "st": st, "IY": iy, "QY": qy,
-        }
-        for step in SCHEDULE:
-            steps[step[0]](*step[1:])
+        interleave(on_vector, ("prev", 0))
+        interleave_b(on_vector, 1, 0)
+        interleave_b(on_vector, 1, 1)
+        multiply_flow(0, 0)
+        empty_flow(0, 0)
+        multiply_flow(0, 1)
+        quantize(("b", 1, 0))
+        quantize(("prev", 0))
+        quantize(("b", 1, 1))
+        empty_flow(0, 1)
+        multiply_flow(1, 0)
+        empty_flow(1, 0)
+        multiply_prev(2)
+        empty_prev(2)
+        interleave_b(on_vector, 2, 0)
+        interleave(on_vector, ("flow", 0, 0))
+        interleave_b(on_vector, 2, 1)
+        quantize(("b", 2, 0))
+        interleave_b(on_vector, 3, 0)
+        quantize(("b", 2, 1))
+        interleave_b(on_vector, 3, 1)
+        quantize(("flow", 0, 0))
+        quantize(("b", 3, 0))
+        interleave(on_vector, ("prev", 1))
+        quantize(("b", 3, 1))
+
+        multiply_flow(2, 0)
+        empty_flow(2, 0)
+        multiply_prev(3)
+        multiply_y(0, 0)
+        empty_prev(3)
+        multiply_flow(3, 0)
+        empty_flow(3, 0)
+        multiply_flow(1, 1)
+        empty_flow(1, 1)
+        interleave(on_vector, ("flow", 1, 0))
+        quantize(("prev", 1))
+        interleave(on_vector, ("flow", 2, 0))
+        quantize(("flow", 1, 0))
+        on_vector(recept[:], recept_in[:])
+        interleave(on_vector, ("prev", 2))
+        quantize(("flow", 2, 0))
+        offset_on_vector(0, 1)
+        quantize(("prev", 2))
+        interleave(on_vector, ("flow", 3, 0))
+        interleave(on_vector, ("prev", 3))
+        quantize(("flow", 3, 0))
+        interleave(on_vector, ("flow", 0, 1))
+        quantize(("prev", 3))
+        multiply_flow(2, 1)
+        empty_flow(2, 1)
+        multiply_flow(3, 1)
+        offset_on_scalar(0, 0)
+        empty_flow(3, 1)
+        for g in range(1, ORIGIN_GROUPS):
+            multiply_y(g, 0)
+        interleave(on_vector, ("flow", 1, 1))
+        quantize(("flow", 0, 1))
+        interleave(on_scalar, ("flow", 2, 1))
+        empty_y(0)
+
+        multiply_y(0, 1)
+        quantize(("flow", 1, 1))
+        interleave(on_scalar, ("flow", 3, 1))
+        interleave(on_vector, ("y", 0), FIRST_HALF)
+        quantize(("flow", 2, 1))
+        interleave(on_vector, ("y", 0), SECOND_HALF)
+        multiply_y(1, 1)
+        multiply_y(2, 1)
+        quantize_y(0, FIRST_HALF)
+        quantize(("flow", 3, 1))
+        quantize_y(0, SECOND_HALF)
+        store_y_scales(0, [nc.sync])
+        offset_on_scalar(1, 0)
+        offset_on_scalar(1, 1)
+        multiply_y(3, 1)
+        empty_y(1)
+        interleave(on_scalar, ("y", 1), SCALAR_SHARE)
+        interleave(on_vector, ("y", 1), VECTOR_SHARE)
+        quantize_y(1, FIRST_HALF)
+        quantize_y(1, SECOND_HALF)
+        store_y_scales(1, [nc.sync, nc.scalar])

@@ -70,7 +70,7 @@ def tile_gravity_mobility_importation_k4_kernel(
         l_scales_in = kept("l_scales_in", [P, O], U8)
         l_scales = kept("l_scales", [P, O], U8)
         a_words = [kept("a_words%d" % d, [P, FEATURE_GROUPS, W], U32) for d in range(DEST_GROUPS)]
-        a_scales = kept("a_scales", [P, FEATURE_GROUPS, D], U8)
+        a_scales = kept("a_scales", [P, D], U8)
         z_rows = kept("z_rows", [P, SLOTS, S], BF16)
         b_early = {(g, c): kept("b_early%d%d" % (g, c), [P, SLOTS, W], BF16) for g in range(2) for c in range(FEATURE_GROUPS)}
         b_late = [kept("b_late%d" % c, [P, SLOTS, 2 * W], BF16) for c in range(FEATURE_GROUPS)]
@@ -110,19 +110,19 @@ def tile_gravity_mobility_importation_k4_kernel(
             nc.sync.dma_start(out=vector_rows[ORIGIN_GROUPS * v : ORIGIN_GROUPS * (v + 1), :],
                               in_=source.rearrange("(g x) -> g x", g=ORIGIN_GROUPS))
         nc.sync.dma_start(out=z_rows[:], in_=drivers.rearrange("(p j) s -> p j s", j=SLOTS))
-        load_b(b_early[0, 0], 0, slice(0, W))
         nc.sync.dma_start(out=l_words_in[:].bitcast(I32), in_=load_words[0].bitcast(I32))
-        for quad in range(4):
-            nc.sync.dma_start(out=l_scales_in[32 * quad : 32 * quad + 4, :].bitcast(I32),
-                              in_=load_scales[0, 4 * quad : 4 * quad + 4, :].bitcast(I32))
+        for r in range(4):
+            nc.sync.dma_start(out=l_scales_in[r:P:32, :].bitcast(I32),
+                              in_=load_scales[0].rearrange("(quad r) n -> r quad n", r=4)[r].bitcast(I32))
+        load_b(b_early[0, 0], 0, slice(0, W))
         load_b(b_early[0, 1], 1, slice(0, W))
         load_a(0)
-        for quad in range(4):
-            nc.sync.dma_start(out=a_scales[32 * quad : 32 * quad + 4, :, :].bitcast(I32),
-                              in_=dest_scales[:, 4 * quad : 4 * quad + 4, :].rearrange("c r n -> r c n").bitcast(I32))
+        for quad in (0, 2, 1, 3):
+            nc.sync.dma_start(out=a_scales[32 * quad : 32 * quad + 8, :].bitcast(I32),
+                              in_=dest_scales[:, 4 * quad : 4 * quad + 4, :].bitcast(I32))
+        load_a(1)
         load_b(b_early[1, 0], 0, slice(W, 2 * W))
         load_b(b_early[1, 1], 1, slice(W, 2 * W))
-        load_a(1)
         load_b(b_late[0], 0, slice(2 * W, O))
         load_b(b_late[1], 1, slice(2 * W, O))
         nc.sync.dma_start(out=recept_in[:], in_=receptivity.rearrange("(d p u) -> p d u", d=DEST_GROUPS, u=SLOTS))
@@ -147,10 +147,10 @@ def tile_gravity_mobility_importation_k4_kernel(
             copy(word_tile(key)[:, cols, :].rearrange("p (n i) t -> p n t i", i=4),
                  by_slot[key][:, :, cols].rearrange("p t (n i) -> p n t i", i=4))
 
-        def interleave_b(copy, g, c, slots=slice(0, SLOTS)):
+        def interleave_b(g, c):
             rows = b_early[g, c][:] if g < 2 else b_late[c][:, :, (g - 2) * W : (g - 1) * W]
-            copy(word_tile(("b", g, c))[:].rearrange("p (t q i) j -> p t q j i", t=SLOTS, i=4)[:, slots],
-                 rows.rearrange("p j (q t i) -> p t q j i", t=SLOTS, i=4)[:, slots])
+            on_vector(word_tile(("b", g, c))[:].rearrange("p (t q i) j -> p t q j i", t=SLOTS, i=4),
+                      rows.rearrange("p j (q t i) -> p t q j i", t=SLOTS, i=4))
 
         def quantize(key, cols=WHOLE):
             nc.vector.quantize_mx(out=codes[key][:, cols].bitcast(FP8X4), scales=scales[key][:, cols],
@@ -221,7 +221,7 @@ def tile_gravity_mobility_importation_k4_kernel(
                 for c in range(FEATURE_GROUPS):
                     nc.tensor.matmul_mx(out=scores[:], lhsT=codes["b", g, c][:, P * t : P * (t + 1)].bitcast(FP8X4),
                                         lhsT_scale=scales["b", g, c][:, P * t : P * (t + 1)],
-                                        rhs=a_words[d][:, c, :].bitcast(FP8X4), rhs_scale=a_scales[:, c, d * W : (d + 1) * W],
+                                        rhs=a_words[d][:, c, :].bitcast(FP8X4), rhs_scale=a_scales[4 * c : P, d * W : (d + 1) * W],
                                         start=(c == 0), stop=(c == FEATURE_GROUPS - 1))
 
         def empty_flow(g, d):
@@ -242,12 +242,7 @@ def tile_gravity_mobility_importation_k4_kernel(
                                     rhs=codes["prev", g][:].bitcast(FP8X4), rhs_scale=scales["prev", g][:],
                                     start=(g == 0), stop=(g == ORIGIN_GROUPS - 1))
 
-        def offset_on_vector(d, pair):
-            for u in (2 * pair, 2 * pair + 1):
-                nc.vector.tensor_scalar(out=offset[:, d, u, :], in0=outside_all[:], scalar1=recept[:, d, u : u + 1],
-                                        scalar2=None, op0=ALU.mult)
-
-        def offset_on_scalar(d, pair):
+        def make_offset(d, pair):
             for u in (2 * pair, 2 * pair + 1):
                 nc.scalar.activation(out=offset[:, d, u, :], in_=outside_all[:], func=ACT.Copy, scale=recept[:, d, u : u + 1])
 
@@ -272,100 +267,97 @@ def tile_gravity_mobility_importation_k4_kernel(
                                                      in_=scales["y", d][32 * quad : 32 * quad + 4, :].bitcast(I32))
 
 
+        interleave(on_scalar, ("z",), FIRST_HALF)
         turn_vectors()
-        interleave(on_scalar, ("z",), SECOND_HALF)
-        interleave(on_vector, ("z",), FIRST_HALF)
+        interleave(on_vector, ("z",), SECOND_HALF)
         mass_mantissa()
-        mass_sign_and_exponent()
         quantize(("z",))
-        interleave_b(on_scalar, 0, 0, slice(2, 4))
         order_l_columns()
         multiply_prev(0)
-        interleave_b(on_vector, 0, 0, slice(0, 2))
-        empty_prev(0)
-        interleave_b(on_vector, 0, 1)
-        quantize(("b", 0, 0))
+        mass_sign_and_exponent()
+        interleave_b(0, 0)
         mass_logarithm()
-        quantize(("b", 0, 1))
+        empty_prev(0)
         multiply_prev(1)
+        quantize(("b", 0, 0))
         empty_prev(1)
-
+        multiply_prev(2)
+        interleave_b(0, 1)
         interleave(on_vector, ("prev", 0))
-        interleave_b(on_vector, 1, 0)
-        interleave_b(on_vector, 1, 1)
+        empty_prev(2)
+        multiply_prev(3)
+        quantize(("b", 0, 1))
+        quantize(("prev", 0))
+        interleave(on_vector, ("prev", 1))
+        empty_prev(3)
         multiply_flow(0, 0)
         empty_flow(0, 0)
         multiply_flow(0, 1)
-        quantize(("b", 1, 0))
-        quantize(("prev", 0))
-        quantize(("b", 1, 1))
         empty_flow(0, 1)
+        quantize(("prev", 1))
+        interleave_b(1, 0)
+        quantize(("b", 1, 0))
+        interleave_b(1, 1)
+        interleave(on_vector, ("prev", 3))
+        quantize(("b", 1, 1))
+        interleave_b(3, 0)
+        interleave_b(2, 0)
         multiply_flow(1, 0)
         empty_flow(1, 0)
-        multiply_prev(2)
-        empty_prev(2)
-        interleave_b(on_vector, 2, 0)
         interleave(on_vector, ("flow", 0, 0))
-        interleave_b(on_vector, 2, 1)
-        quantize(("b", 2, 0))
-        interleave_b(on_vector, 3, 0)
-        quantize(("b", 2, 1))
-        interleave_b(on_vector, 3, 1)
-        quantize(("flow", 0, 0))
-        quantize(("b", 3, 0))
-        interleave(on_vector, ("prev", 1))
-        quantize(("b", 3, 1))
-
-        multiply_flow(2, 0)
-        empty_flow(2, 0)
-        multiply_prev(3)
-        multiply_y(0, 0)
-        empty_prev(3)
-        multiply_flow(3, 0)
-        empty_flow(3, 0)
         multiply_flow(1, 1)
+        interleave_b(2, 1)
         empty_flow(1, 1)
+        quantize(("b", 2, 0))
+        quantize(("b", 2, 1))
+        interleave_b(3, 1)
+        quantize(("b", 3, 0))
+        quantize(("b", 3, 1))
         interleave(on_vector, ("flow", 1, 0))
-        quantize(("prev", 1))
-        interleave(on_vector, ("flow", 2, 0))
-        quantize(("flow", 1, 0))
-        on_vector(recept[:], recept_in[:])
-        interleave(on_vector, ("prev", 2))
-        quantize(("flow", 2, 0))
-        offset_on_vector(0, 1)
-        quantize(("prev", 2))
-        interleave(on_vector, ("flow", 3, 0))
-        interleave(on_vector, ("prev", 3))
-        quantize(("flow", 3, 0))
         interleave(on_vector, ("flow", 0, 1))
-        quantize(("prev", 3))
-        multiply_flow(2, 1)
-        empty_flow(2, 1)
-        multiply_flow(3, 1)
-        offset_on_scalar(0, 0)
-        empty_flow(3, 1)
-        for g in range(1, ORIGIN_GROUPS):
-            multiply_y(g, 0)
-        interleave(on_vector, ("flow", 1, 1))
+        multiply_flow(2, 0)
+        quantize(("flow", 1, 0))
+        interleave(on_vector, ("prev", 2))
+        empty_flow(2, 0)
+        quantize(("flow", 0, 0))
+        interleave(on_vector, ("flow", 2, 0))
+        multiply_flow(3, 0)
+        quantize(("prev", 2))
+        quantize(("flow", 2, 0))
+        empty_flow(3, 0)
         quantize(("flow", 0, 1))
-        interleave(on_scalar, ("flow", 2, 1))
+        multiply_flow(2, 1)
+        interleave(on_vector, ("flow", 3, 0))
+        multiply_y(0, 0)
+        empty_flow(2, 1)
+        on_scalar(recept[:], recept_in[:])
+        make_offset(0, 0)
+        multiply_flow(3, 1)
+        quantize(("prev", 3))
+        multiply_y(1, 0)
+        multiply_y(2, 0)
+        quantize(("flow", 3, 0))
+        interleave(on_vector, ("flow", 1, 1))
+        empty_flow(3, 1)
+        multiply_y(3, 0)
+        make_offset(0, 1)
         empty_y(0)
-
-        multiply_y(0, 1)
         quantize(("flow", 1, 1))
-        interleave(on_scalar, ("flow", 3, 1))
-        interleave(on_vector, ("y", 0), FIRST_HALF)
+        multiply_y(0, 1)
+        interleave(on_scalar, ("flow", 2, 1))
         quantize(("flow", 2, 1))
-        interleave(on_vector, ("y", 0), SECOND_HALF)
+        interleave(on_vector, ("y", 0), FIRST_HALF)
+        interleave(on_scalar, ("flow", 3, 1))
         multiply_y(1, 1)
         multiply_y(2, 1)
-        quantize_y(0, FIRST_HALF)
+        interleave(on_vector, ("y", 0), SECOND_HALF)
+        make_offset(1, 0)
         quantize(("flow", 3, 1))
         quantize_y(0, SECOND_HALF)
+        quantize_y(0, FIRST_HALF)
         store_y_scales(0, [nc.sync])
-        offset_on_scalar(1, 0)
-        offset_on_scalar(1, 1)
         multiply_y(3, 1)
+        make_offset(1, 1)
         empty_y(1)
         interleave(on_scalar, ("y", 1), SCALAR_SHARE)
         interleave(on_vector, ("y", 1), VECTOR_SHARE)

from contextlib import ExitStack

import concourse.mybir as mybir
from concourse.masks import make_identity

D, O, S, K, C = 1024, 2048, 512, 1024, 512
FLOPS = 2 * D * O * K + 2 * O * S * C + 2 * D * S * O

F32 = mybir.dt.float32
BF16 = mybir.dt.bfloat16
I32 = mybir.dt.int32
U32 = mybir.dt.uint32
U8 = mybir.dt.uint8
FP8X4 = mybir.dt.float8_e4m3fn_x4
FP4X4 = mybir.dt.float4_e2m1fn_x4
ACT = mybir.ActivationFunctionType
ALU = mybir.AluOpType

P = 128
W = 512
SLOTS = 4
ORIGIN_GROUPS = O // W
DEST_GROUPS = D // W
FEATURE_GROUPS = K // W
VECTOR_ROWS = 3 * ORIGIN_GROUPS
WORD_BUFS = 7
SLOT_BUFS = 10
LN2 = 0.6931471805599453
ZERO_MASS_EXPONENT = -1.0e4

WHOLE = slice(0, W)
FIRST_HALF = slice(0, W // 2)
SECOND_HALF = slice(W // 2, W)
VECTOR_SHARE = slice(0, 3 * W // 4)
SCALAR_SHARE = slice(3 * W // 4, W)


def tile_gravity_mobility_importation_k4_kernel(
    tc, dest_words, dest_scales, origin_feat, load_words, load_scales, drivers,
    mass, amplitude, common, outside, receptivity, out_0, out_1, out_2,
):
    nc = tc.nc
    with ExitStack() as ctx:
        keep = ctx.enter_context(tc.tile_pool(name="keep", bufs=1))
        staging = ctx.enter_context(tc.tile_pool(name="staging", bufs=1))
        psum = ctx.enter_context(tc.psum_pool(name="psum", bufs=1))
        ctx.enter_context(tc.manual_schedule())

        def kept(name, shape, dtype):
            return keep.tile(shape, dtype, name=name, align_bytes=64)

        vector_rows = kept("vector_rows", [VECTOR_ROWS, W], BF16)
        vector_rows_by_slot = kept("vector_rows_by_slot", [P, SLOTS, P], BF16)
        ident = kept("ident", [P, P], BF16)
        per_origin = kept("per_origin", [P, 3, 16], F32)
        mantissa = kept("mantissa", [P, 16], I32)
        exponent_bits = kept("exponent_bits", [P, 16], I32)
        twice_nonneg = kept("twice_nonneg", [P, 16], F32)
        signed = kept("signed", [P, 2, 16], F32)
        exponent = kept("exponent", [P, 16], F32)
        zero_shift = kept("zero_shift", [P, 16], F32)
        ln_mantissa = kept("ln_mantissa", [P, 16], F32)
        ln_mass = kept("ln_mass", [P, 16], F32)
        recept_in = kept("recept_in", [P, DEST_GROUPS, SLOTS], BF16)
        recept = kept("recept", [P, DEST_GROUPS, SLOTS], F32)
        outside_all = kept("outside_all", [P, S], BF16)
        offset = kept("offset", [P, DEST_GROUPS, SLOTS, S], F32)
        l_words_in = kept("l_words_in", [P, 2 * O], U8)
        l_words = kept("l_words", [P, 2 * O], U8)
        l_scales_in = kept("l_scales_in", [P, O], U8)
        l_scales = kept("l_scales", [P, O], U8)
        a_words = [kept("a_words%d" % d, [P, FEATURE_GROUPS, W], U32) for d in range(DEST_GROUPS)]
        a_scales = kept("a_scales", [P, D], U8)
        z_rows = kept("z_rows", [P, SLOTS, S], BF16)
        b_early = {(g, c): kept("b_early%d%d" % (g, c), [P, SLOTS, W], BF16) for g in range(2) for c in range(FEATURE_GROUPS)}
        b_late = [kept("b_late%d" % c, [P, SLOTS, 2 * W], BF16) for c in range(FEATURE_GROUPS)]
        warm = kept("warm", [P, 1], F32)
        warm_ln = kept("warm_ln", [P, 1], F32)
        warm_exp = kept("warm_exp", [P, 1], F32)
        y = [kept("y%d" % d, [P, SLOTS, S], F32) for d in range(DEST_GROUPS)]

        keys = [("z",)]
        keys += [("b", g, c) for g in range(ORIGIN_GROUPS) for c in range(FEATURE_GROUPS)]
        keys += [("prev", g) for g in range(ORIGIN_GROUPS)]
        keys += [("flow", g, d) for g in range(ORIGIN_GROUPS) for d in range(DEST_GROUPS)]
        keys += [("y", d) for d in range(DEST_GROUPS)]
        codes = {key: kept("codes_" + "".join(map(str, key)), [P, W], U32) for key in keys}
        scales = {key: kept("scales_" + "".join(map(str, key)), [P, W], U8) for key in keys}
        by_slot = {("z",): z_rows, ("y", 0): y[0], ("y", 1): y[1]}
        by_word = {}
        bank = {}

        nc.gpsimd.memset(vector_rows_by_slot[:].rearrange("p t m -> p (t m)").bitcast(I32), 0)
        nc.gpsimd.memset(warm[:], 1.0)
        nc.vector.memset(l_scales_in[:].bitcast(I32), 0)
        make_identity(nc, ident[:])
        nc.gpsimd.memset(a_scales[:].bitcast(I32), 0)
        nc.scalar.activation(out=warm_ln[:], in_=warm[:], func=ACT.Ln)

        def load_b(tile, c, origins):
            nc.sync.dma_start(out=tile[:], in_=origin_feat[c * W : (c + 1) * W, origins].rearrange("(p j) o -> p j o", j=SLOTS))

        def load_a(d):
            nc.sync.dma_start(
                out=a_words[d][:].bitcast(I32),
                in_=dest_words.rearrange("c p n j -> p c (n j)")[:, :, d * SLOTS * W : (d + 1) * SLOTS * W].bitcast(I32),
            )

        for v, source in enumerate((mass, amplitude, common)):
            nc.sync.dma_start(out=vector_rows[ORIGIN_GROUPS * v : ORIGIN_GROUPS * (v + 1), :],
                              in_=source.rearrange("(g x) -> g x", g=ORIGIN_GROUPS))
        nc.sync.dma_start(out=z_rows[:], in_=drivers.rearrange("(p j) s -> p j s", j=SLOTS))
        nc.sync.dma_start(out=l_words_in[:].bitcast(I32), in_=load_words[0].bitcast(I32))
        for r in range(4):
            nc.sync.dma_start(out=l_scales_in[r:P:32, :].bitcast(I32),
                              in_=load_scales[0].rearrange("(quad r) n -> r quad n", r=4)[r].bitcast(I32))
        load_b(b_early[0, 0], 0, slice(0, W))
        load_b(b_early[0, 1], 1, slice(0, W))
        load_a(0)
        for quad in (0, 2, 1, 3):
            nc.sync.dma_start(out=a_scales[32 * quad : 32 * quad + 8, :].bitcast(I32),
                              in_=dest_scales[:, 4 * quad : 4 * quad + 4, :].bitcast(I32))
        load_a(1)
        load_b(b_early[1, 0], 0, slice(W, 2 * W))
        load_b(b_early[1, 1], 1, slice(W, 2 * W))
        load_b(b_late[0], 0, slice(2 * W, O))
        load_b(b_late[1], 1, slice(2 * W, O))
        nc.sync.dma_start(out=recept_in[:], in_=receptivity.rearrange("(d p u) -> p d u", d=DEST_GROUPS, u=SLOTS))
        nc.sync.dma_start(out=outside_all[:], in_=outside.partition_broadcast(P))

        def on_vector(out, in_):
            nc.vector.tensor_copy(out=out, in_=in_)

        def on_scalar(out, in_):
            nc.scalar.copy(out=out, in_=in_)

        def word_tile(key):
            if key not in by_word:
                by_word[key] = staging.tile([P, W, SLOTS], BF16, name="by_word", tag="by_word", bufs=WORD_BUFS, align_bytes=64)
            return by_word[key]

        def slot_tile(key):
            by_slot[key] = staging.tile([P, SLOTS, W], BF16, name="by_slot", tag="by_slot", bufs=SLOT_BUFS, align_bytes=64)
            return by_slot[key]

        def interleave(copy, key, cols=WHOLE):
            copy(word_tile(key)[:, cols, :].rearrange("p (n i) t -> p n t i", i=4),
                 by_slot[key][:, :, cols].rearrange("p t (n i) -> p n t i", i=4))

        def interleave_b(g, c):
            rows = b_early[g, c][:] if g < 2 else b_late[c][:, :, (g - 2) * W : (g - 1) * W]
            on_vector(word_tile(("b", g, c))[:].rearrange("p (t q i) j -> p t q j i", t=SLOTS, i=4),
                      rows.rearrange("p j (q t i) -> p t q j i", t=SLOTS, i=4))

        def quantize(key, cols=WHOLE):
            nc.vector.quantize_mx(out=codes[key][:, cols].bitcast(FP8X4), scales=scales[key][:, cols],
                                  in_=by_word[key][:, cols, :].rearrange("p n t -> p (n t)"))

        def turn_vectors():
            nc.vector.tensor_copy(out=vector_rows_by_slot[0:VECTOR_ROWS].rearrange("r t (q i) -> r t q i", i=4),
                                  in_=vector_rows[:].rearrange("r (q t i) -> r t q i", t=SLOTS, i=4))
            bank["vectors"] = psum.tile([P, SLOTS, P], BF16, name="vectors", tag="sum0")
            for t in range(SLOTS):
                nc.tensor.transpose(bank["vectors"][:, t, :], vector_rows_by_slot[:, t, :], ident[:])

        def mass_mantissa():
            nc.vector.tensor_copy(out=per_origin[:].rearrange("p v (t g) -> p v t g", g=ORIGIN_GROUPS),
                                  in_=bank["vectors"][:, :, 0:VECTOR_ROWS].rearrange("p t (v g) -> p v t g", g=ORIGIN_GROUPS))
            nc.vector.tensor_scalar(out=mantissa[:], in0=per_origin[:, 0, :].bitcast(I32), scalar1=0x007FFFFF,
                                    scalar2=0x3F800000, op0=ALU.bitwise_and, op1=ALU.bitwise_or)
            nc.scalar.activation(out=ln_mantissa[:], in_=mantissa[:].bitcast(F32), func=ACT.Ln)
            nc.scalar.activation(out=warm_exp[:], in_=warm[:], func=ACT.Exp)

        def mass_sign_and_exponent():
            nc.vector.tensor_scalar(out=twice_nonneg[:], in0=per_origin[:, 0, :], scalar1=0.0, scalar2=2.0,
                                    op0=ALU.is_ge, op1=ALU.mult)
            nc.vector.tensor_scalar(out=exponent_bits[:], in0=per_origin[:, 0, :].bitcast(I32), scalar1=23, scalar2=0xFF,
                                    op0=ALU.logical_shift_right, op1=ALU.bitwise_and)
            nc.vector.tensor_scalar(out=zero_shift[:], in0=per_origin[:, 0, :], scalar1=0.0, scalar2=ZERO_MASS_EXPONENT,
                                    op0=ALU.is_equal, op1=ALU.mult)
            for v in range(2):
                nc.vector.scalar_tensor_tensor(out=signed[:, v, :], in0=twice_nonneg[:], scalar=-1.0,
                                               in1=per_origin[:, 1 + v, :], op0=ALU.add, op1=ALU.mult)
            nc.vector.scalar_tensor_tensor(out=exponent[:], in0=exponent_bits[:], scalar=-127.0, in1=zero_shift[:],
                                           op0=ALU.add, op1=ALU.add)

        def mass_logarithm():
            nc.vector.scalar_tensor_tensor(out=ln_mass[:], in0=exponent[:], scalar=LN2, in1=ln_mantissa[:],
                                           op0=ALU.mult, op1=ALU.add)

        def order_l_columns():
            nc.vector.tensor_copy(
                out=l_words[:].bitcast(I32).rearrange("p (g t q w) -> p g t q w", g=ORIGIN_GROUPS, t=SLOTS, w=2),
                in_=l_words_in[:].bitcast(I32).rearrange("p (g q t w) -> p g t q w", g=ORIGIN_GROUPS, t=SLOTS, w=2))
            nc.vector.tensor_copy(
                out=l_scales[:].bitcast(I32).rearrange("p (g t q) -> p g t q", g=ORIGIN_GROUPS, t=SLOTS),
                in_=l_scales_in[:].bitcast(I32).rearrange("p (g q t) -> p g t q", g=ORIGIN_GROUPS, t=SLOTS))

        def first_stage_bank(key, t):
            bank[key, t] = psum.tile([P, W], F32, name="first", tag="first%d" % t)
            return bank[key, t]

        def multiply_prev(g):
            for t in range(SLOTS):
                n = SLOTS * g + t
                nc.tensor.matmul_mx(out=first_stage_bank(("prev", g), t)[:],
                                    lhsT=l_words[:, 2 * P * n : 2 * P * (n + 1)].bitcast(FP4X4),
                                    lhsT_scale=l_scales[:, P * n : P * (n + 1)],
                                    rhs=codes["z",][:].bitcast(FP8X4), rhs_scale=scales["z",][:], start=True, stop=True)

        def empty_prev(g):
            rows = slot_tile(("prev", g))
            for t in range(SLOTS):
                n = ORIGIN_GROUPS * t + g
                nc.scalar.activation(out=rows[:, t, :], in_=bank[("prev", g), t][:], func=ACT.Identity,
                                     scale=signed[:, 0, n : n + 1], bias=signed[:, 1, n : n + 1])

        def multiply_flow(g, d):
            for t in range(SLOTS):
                scores = first_stage_bank(("flow", g, d), t)
                for c in range(FEATURE_GROUPS):
                    nc.tensor.matmul_mx(out=scores[:], lhsT=codes["b", g, c][:, P * t : P * (t + 1)].bitcast(FP8X4),
                                        lhsT_scale=scales["b", g, c][:, P * t : P * (t + 1)],
                                        rhs=a_words[d][:, c, :].bitcast(FP8X4), rhs_scale=a_scales[4 * c : P, d * W : (d + 1) * W],
                                        start=(c == 0), stop=(c == FEATURE_GROUPS - 1))

        def empty_flow(g, d):
            rows = slot_tile(("flow", g, d))
            for t in range(SLOTS):
                n = ORIGIN_GROUPS * t + g
                nc.scalar.activation(out=rows[:, t, :].rearrange("p (u m) -> p u m", u=SLOTS),
                                     in_=bank[("flow", g, d), t][:].rearrange("p (m u) -> p u m", u=SLOTS),
                                     func=ACT.Exp, bias=ln_mass[:, n : n + 1])

        def multiply_y(g, d):
            for u in range(SLOTS):
                if g == 0:
                    bank[("y", d), u] = psum.tile([P, S], F32, name="sum", tag="sum%d" % u)
                nc.tensor.matmul_mx(out=bank[("y", d), u][:],
                                    lhsT=codes["flow", g, d][:, P * u : P * (u + 1)].bitcast(FP8X4),
                                    lhsT_scale=scales["flow", g, d][:, P * u : P * (u + 1)],
                                    rhs=codes["prev", g][:].bitcast(FP8X4), rhs_scale=scales["prev", g][:],
                                    start=(g == 0), stop=(g == ORIGIN_GROUPS - 1))

        def make_offset(d, pair):
            for u in (2 * pair, 2 * pair + 1):
                nc.scalar.activation(out=offset[:, d, u, :], in_=outside_all[:], func=ACT.Copy, scale=recept[:, d, u : u + 1])

        def empty_y(d):
            for pair in range(2):
                for u in (2 * pair, 2 * pair + 1):
                    nc.vector.scalar_tensor_tensor(out=y[d][:, u, :], in0=bank[("y", d), u][:], scalar=recept[:, d, u : u + 1],
                                                   in1=offset[:, d, u, :], op0=ALU.mult, op1=ALU.add)
                nc.sync.dma_start(
                    out=out_0[d * W : (d + 1) * W, :].rearrange("(p u) s -> p u s", u=SLOTS)[:, 2 * pair : 2 * pair + 2, :],
                    in_=y[d][:, 2 * pair : 2 * pair + 2, :])

        def quantize_y(d, cols):
            quantize(("y", d), cols)
            nc.sync.dma_start(
                out=out_1[d].rearrange("p s u -> p (s u)")[:, SLOTS * cols.start : SLOTS * cols.stop].bitcast(I32),
                in_=codes["y", d][:, cols].bitcast(I32))

        def store_y_scales(d, queues):
            for quad in range(4):
                queues[quad % len(queues)].dma_start(out=out_2[d, 4 * quad : 4 * quad + 4, :].bitcast(I32),
                                                     in_=scales["y", d][32 * quad : 32 * quad + 4, :].bitcast(I32))


        interleave(on_scalar, ("z",), FIRST_HALF)
        turn_vectors()
        interleave(on_vector, ("z",), SECOND_HALF)
        mass_mantissa()
        quantize(("z",))
        order_l_columns()
        multiply_prev(0)
        mass_sign_and_exponent()
        interleave_b(0, 0)
        mass_logarithm()
        empty_prev(0)
        multiply_prev(1)
        quantize(("b", 0, 0))
        empty_prev(1)
        multiply_prev(2)
        interleave_b(0, 1)
        interleave(on_vector, ("prev", 0))
        empty_prev(2)
        multiply_prev(3)
        quantize(("b", 0, 1))
        quantize(("prev", 0))
        interleave(on_vector, ("prev", 1))
        empty_prev(3)
        multiply_flow(0, 0)
        empty_flow(0, 0)
        multiply_flow(0, 1)
        empty_flow(0, 1)
        quantize(("prev", 1))
        interleave_b(1, 0)
        quantize(("b", 1, 0))
        interleave_b(1, 1)
        interleave(on_vector, ("prev", 3))
        quantize(("b", 1, 1))
        interleave_b(3, 0)
        interleave_b(2, 0)
        multiply_flow(1, 0)
        empty_flow(1, 0)
        interleave(on_vector, ("flow", 0, 0))
        multiply_flow(1, 1)
        interleave_b(2, 1)
        empty_flow(1, 1)
        quantize(("b", 2, 0))
        quantize(("b", 2, 1))
        interleave_b(3, 1)
        quantize(("b", 3, 0))
        quantize(("b", 3, 1))
        interleave(on_vector, ("flow", 1, 0))
        interleave(on_vector, ("flow", 0, 1))
        multiply_flow(2, 0)
        quantize(("flow", 1, 0))
        interleave(on_vector, ("prev", 2))
        empty_flow(2, 0)
        quantize(("flow", 0, 0))
        interleave(on_vector, ("flow", 2, 0))
        multiply_flow(3, 0)
        quantize(("prev", 2))
        quantize(("flow", 2, 0))
        empty_flow(3, 0)
        quantize(("flow", 0, 1))
        multiply_flow(2, 1)
        interleave(on_vector, ("flow", 3, 0))
        multiply_y(0, 0)
        empty_flow(2, 1)
        on_scalar(recept[:], recept_in[:])
        make_offset(0, 0)
        multiply_flow(3, 1)
        quantize(("prev", 3))
        multiply_y(1, 0)
        multiply_y(2, 0)
        quantize(("flow", 3, 0))
        interleave(on_vector, ("flow", 1, 1))
        empty_flow(3, 1)
        multiply_y(3, 0)
        make_offset(0, 1)
        empty_y(0)
        quantize(("flow", 1, 1))
        multiply_y(0, 1)
        interleave(on_scalar, ("flow", 2, 1))
        quantize(("flow", 2, 1))
        interleave(on_vector, ("y", 0), FIRST_HALF)
        interleave(on_scalar, ("flow", 3, 1))
        multiply_y(1, 1)
        multiply_y(2, 1)
        interleave(on_vector, ("y", 0), SECOND_HALF)
        make_offset(1, 0)
        quantize(("flow", 3, 1))
        quantize_y(0, SECOND_HALF)
        quantize_y(0, FIRST_HALF)
        store_y_scales(0, [nc.sync])
        multiply_y(3, 1)
        make_offset(1, 1)
        empty_y(1)
        interleave(on_scalar, ("y", 1), SCALAR_SHARE)
        interleave(on_vector, ("y", 1), VECTOR_SHARE)
        quantize_y(1, FIRST_HALF)
        quantize_y(1, SECOND_HALF)
        store_y_scales(1, [nc.sync, nc.scalar])
